import numpy as np
CORES = [100,101,102,103,108,109,110,111]
N = 8
RM, R, T = 262144, 8192, 4096
CAPP = 1024
def entries(a): return a.T.reshape(-1)
def pack(v, P): return np.ascontiguousarray(np.asarray(v, np.int32).reshape(-1, P).T)
def owners(rng, how):
    if how == "alike": return np.stack([rng.permutation(np.repeat(rng.permutation(N)[:T // CAPP], CAPP)) for r in range(N)])
    if how == "full": p = np.repeat(rng.permutation(N)[:T // CAPP], CAPP); return np.stack([rng.permutation(p) for r in range(N)])
    return np.stack([rng.permutation(np.repeat(np.arange(N), CAPP))[:T] for r in range(N)])
def lists(rng, how):
    M = rng.integers(0, N * R, N * RM)
    O1 = owners(rng, how); O2 = rng.permutation(N)[O1] if how in ("alike", "full") else owners(rng, "uniform")
    sl = np.stack([1 + rng.permutation(RM - 2)[:N * T] for o in range(N)])
    if how == "edge": sl[:, 0] = 0; sl[:, 1] = RM - 1
    I = np.zeros((N, T), np.int64); took = np.zeros(N, np.int64)
    for r in range(N):
        for o in range(N): m = np.nonzero(O1[r] == o)[0]; I[r, m] = RM * o + sl[o, took[o]:took[o] + len(m)]; took[o] += len(m)
    A = R * O2 + (np.where(rng.random((N, T)) < 0.5, 0, R - 1) if how == "edge" else rng.integers(0, R, (N, T)))
    if how == "alike": I = RM * O1 + sl[O1, 0]; A = R * O2 + rng.integers(0, R, N)[O1]
    M[I.reshape(-1)] = A.reshape(-1)
    if how == "sorted": I = np.sort(I, axis=1)
    if how == "full":
        I[1::3] = np.sort(I[1::3], axis=1); I[2::3] = np.sort(I[2::3], axis=1).reshape(-1, 16, T // 16).transpose(0, 2, 1).reshape(-1, T)
    return {"mp": np.stack([pack(m, 16) for m in M.reshape(N, RM)]), "idx": np.stack([pack(i, 16) for i in I])}
def setup_inputs(rng):
    return dict({"tab": rng.standard_normal((N, 128, R), dtype=np.float32)}, **lists(rng, "uniform"))
def setup_inputs_alike(rng):
    d = setup_inputs(rng); d.update(lists(rng, "alike"))
    for k in ("tab",): d[k] = (d[k].astype(np.float32) * 1048576.0).astype(d[k].dtype)
    return d
def setup_inputs_edge(rng):
    d = setup_inputs(rng); d.update(lists(rng, "edge"))
    for k in ("tab",): d[k] = (d[k].astype(np.float32) * (1 / 1024.0)).astype(d[k].dtype)
    return d
def setup_inputs_full(rng):
    d = setup_inputs(rng); d.update(lists(rng, "full"))
    return d
def setup_inputs_sorted(rng):
    d = setup_inputs(rng); d.update(lists(rng, "sorted"))
    return d
def check_inputs(x):
    bad = []
    if x["mp"].min() < 0 or x["mp"].max() >= N * R: bad.append("mp out of range")
    if x["idx"].min() < 0 or x["idx"].max() >= N * RM: bad.append("idx out of range")
    M = np.concatenate([entries(m) for m in x["mp"]])
    if max(int(np.bincount(entries(a) // RM, minlength=N).max()) for a in x["idx"]) > CAPP: bad.append("more than CAPP entries of a list point into one rank's part of the map")
    if max(int(np.bincount(M[entries(a)] // R, minlength=N).max()) for a in x["idx"]) > CAPP: bad.append("more than CAPP entries of a list have map values in one rank's part of the table")
    return bad
def reference(tab, mp, idx):
    A = np.concatenate(list(tab), axis=1)
    M = np.concatenate([entries(m) for m in mp])
    return {"y": np.stack([A[:, M[entries(idx[r])]] for r in range(N)])}

@@ -1,0 +1,416 @@
+from concourse.bass import DstId, RemoteDMATransfer
+from concourse.mybir import AluOpType, ActivationFunctionType
+
+SIM = 112
+NP = 2
+Z = 8192
+
+SCRATCH = {
+    "lst": ("sbuf", [128, 256], "int32"),
+    "lsf": ("sbuf", [128, 256], "int32"),
+    "win": ("sbuf", [128, 8196], "int32"),
+    "pi": ("sbuf", [128, 5], "int32"),
+    "pf": ("sbuf", [128, 4], "float32"),
+    "offe": ("sbuf", [128, 2], "uint16"),
+    "it16": ("sbuf", [128, 16], "float32"),
+    "smat": ("sbuf", [128, 16], "float32"),
+    "rs16": ("sbuf", [128, 256], "float32"),
+    "ti": ("sbuf", [128, 768], "int32"),
+    "tf": ("sbuf", [128, 1024], "float32"),
+    "off1": ("sbuf", [128, 256], "uint16"),
+    "ei": ("sbuf", [128, 32], "int32"),
+    "em": ("sbuf", [128, 32], "int32"),
+    "oh": ("sbuf", [128, 512], "float32"),
+    "gat": ("sbuf", [128, 4096], "float32"),
+    "xm": ("sbuf", [128, 512], "float32"),
+    "xs": ("sbuf", [128, 512], "float32"),
+    "res": ("sbuf", [128, 32], "float32"),
+    "ra": ("sbuf", [128, 32], "float32"),
+    "rb": ("sbuf", [128, 32], "float32"),
+    "it128": ("sbuf", [128, 128], "bfloat16"),
+    "ones": ("sbuf", [128, 1024], "bfloat16"),
+    "neg": ("sbuf", [128, 128], "bfloat16"),
+    "tri": ("sbuf", [128, 128], "bfloat16"),
+    "base": ("sbuf", [1, 256], "bfloat16"),
+    "rs32": ("sbuf", [128, 256], "bfloat16"),
+    "rep": ("sbuf", [128, 1024], "bfloat16"),
+    "rep7": ("sbuf", [128, 1024], "bfloat16"),
+    "vi": ("sbuf", [128, 32], "int32"),
+    "o2": ("sbuf", [128, 32], "int32"),
+    "ib": ("sbuf", [128, 128], "int32"),
+    "fb": ("sbuf", [128, 128], "float32"),
+    "msk": ("sbuf", [128, 256], "bfloat16"),
+    "scn": ("sbuf", [128, 256], "bfloat16"),
+    "pm": ("sbuf", [128, 256], "float32"),
+    "ss": ("sbuf", [128, 192], "float32"),
+    "pos": ("sbuf", [128, 32], "int32"),
+    "lhs": ("sbuf", [128, 4096], "bfloat16"),
+    "rhs": ("sbuf", [128, 4096], "bfloat16"),
+    "LL": ("sbuf", [128, 1024], "bfloat16"),
+    "qi": ("sbuf", [128, 128], "int32"),
+    "qf": ("sbuf", [128, 64], "float32"),
+    "qb": ("sbuf", [128, 64], "bfloat16"),
+    "off2": ("sbuf", [128, 256], "uint16"),
+    "tw": ("sbuf", [128, 8192], "float32"),
+    "offr": ("sbuf", [128, 512], "uint16"),
+    "og": ("sbuf", [128, 7168], "float32"),
+    "land": ("sbuf", [128, 8192], "float32"),
+    "rly": ("sbuf", [128, 4096], "float32"),
+    "yb": ("sbuf", [128, 4096], "float32"),
+    "pv0": ("psum", [128, 512], "float32"),
+    "pv1": ("psum", [128, 512], "float32"),
+    "prk": ("psum", [128, 512], "float32"),
+    "pl": ("psum", [128, 512], "float32"),
+    "pr0": ("psum", [128, 512], "float32"),
+    "pr1": ("psum", [128, 512], "float32"),
+    "pr2": ("psum", [128, 512], "float32"),
+    "pr3": ("psum", [128, 512], "float32"),
+}
+SEMAPHORES = (["cv", "ct", "ca", "cp", "dix", "dm0", "dm1", "dtab", "dy", "lst", "lsf", "rh", "rf", "off2", "ls", "ms"]
+              + ["m%d%d" % (i, h) for i in range(4) for h in range(NP)]
+              + ["L%d" % r for r in range(8)] + ["d%d" % r for r in range(8)] + ["rl%d" % r for r in range(5)])
+
+
+def _lanes(cores, chip, topo):
+    far = [c for c in cores if topo.chip(c) != chip]
+    idle = [c for c in range(SIM) if topo.chip(c) == chip and c not in cores]
+    port = {c: all(topo.may_write(c, d) for d in far) for c in range(SIM) if topo.chip(c) == chip}
+    with_port = [c for c in idle if port[c]]
+    without = [c for c in idle if not port[c]]
+    out = []
+    for c in cores:
+        if topo.chip(c) != chip:
+            continue
+        q = without.pop(0) if port[c] else with_port.pop(0)
+        out.append({"R": c, "Q": q, "S": c if port[c] else q, "H": q if port[c] else c})
+    return out
+
+
+def rank_program(g, core, T, topo):
+    A = AluOpType
+    cores = list(T.cores)
+    chips = []
+    for c in cores:
+        if topo.chip(c) not in chips:
+            chips.append(topo.chip(c))
+    if topo.chip(core) not in chips:
+        return
+    gi = chips.index(topo.chip(core))
+    lanes = _lanes(cores, chips[gi], topo)
+    flanes = _lanes(cores, chips[1 - gi], topo)
+    mine = [i for i in range(len(lanes)) if core in (lanes[i]["R"], lanes[i]["Q"])]
+    if not mine:
+        return
+    li = mine[0]
+    me, fl = lanes[li], flanes[li]
+    nl = len(lanes)
+    is_rank = core == me["R"]
+    is_sorter = core == me["S"]
+    near_r = [cores.index(l["R"]) for l in lanes]
+    far_r = [cores.index(l["R"]) for l in flanes]
+    myr = cores.index(me["R"])
+    on_mask = topo.mask(me["R"], me["Q"])
+    off_mask = topo.mask(me["S"], fl["S"])
+
+    queues = {"v": g.vector, "t": g.tensor, "a": g.scalar, "p": g, "s": g.sync}
+    cnt = {"cv": 0, "ct": 0, "ca": 0, "cp": 0, "ls": 0, "ms": 0}
+    seen = {}
+
+    def bits(m):
+        return bin(m).count("1")
+
+    def wait(q, *toks):
+        for tok in toks:
+            if tok is None:
+                continue
+            sem, val = tok
+            if seen.get((q, sem), 0) < val:
+                queues[q].wait_ge(T.sem[sem], val)
+                seen[(q, sem)] = val
+
+    def op(q, deps, f):
+        wait(q, *deps)
+        s = "c" + q
+        f().then_inc(T.sem[s], 1)
+        cnt[s] += 1
+        return (s, cnt[s])
+
+    def send(dsts, out, src, rsem, mask, lsem="ls"):
+        if len(dsts) == 1:
+            rid, pid, _ = topo.addr(dsts[0])
+            g.remote_dma(out, src, T.sem[rsem], T.sem[lsem], pid, rid, mask)
+        else:
+            ids = []
+            for d in dsts:
+                rid, pid, _ = topo.addr(d)
+                ids.append(DstId(rid=rid, pnc=pid))
+            g.remote_dma_fused([RemoteDMATransfer(dst_ids=ids, dma_engine_mask=mask, remote_sem=T.sem[rsem],
+                                                  srcs=[src], dsts=[out] * len(dsts))], local_sem=T.sem[lsem])
+        cnt[lsem] += bits(mask)
+
+    V, S = g.vector, g.scalar
+
+    def ts(out, in0, s1, s2, o0, o1=None):
+        if o1 is None:
+            return V.tensor_scalar(out, in0, s1, s2, o0)
+        return V.tensor_scalar(out, in0, s1, s2, o0, o1)
+
+    dma_tot = {}
+
+    def dma(q, sem, out, in_):
+        queues[q].dma_start(out, in_).then_inc(T.sem[sem], 16)
+        dma_tot[sem] = dma_tot.get(sem, 0) + 16
+        return (sem, dma_tot[sem])
+
+    hw = 16384 // NP
+    pw = 2048 // NP
+    if is_rank:
+        for k in range(8):
+            tok_idx = dma("s" if k % 2 == 0 else "a", "dix", T.lst[16 * k:16 * k + 16, :], T.idx[:])
+        tok_map = []
+        for h in range(NP):
+            c0 = 2048 * li + pw * h
+            tok_map.append(dma("s", "dm%d" % h, T.win[:, c0:c0 + pw], T.mp[:, hw * h:hw * h + hw]))
+
+    k_pcol = op("p", [], lambda: g.iota(T.pi[:, 2:3], [[0, 1]], 0, 1))
+    k_it2 = op("p", [], lambda: g.iota(T.pi[:, 3:5], [[128, 2]], 0, 0))
+    k_it16 = op("p", [], lambda: g.iota(T.it16[:], [[1, 16]], 0, 0, allow_small_or_imprecise_dtypes=True))
+    k_z = op("v", [], lambda: V.memset(T.win[:, Z:Z + 4], 0))
+    k_r = op("v", [], lambda: V.memset(T.rs16[:], 1.0))
+    k_a = op("v", [k_pcol], lambda: ts(T.pi[:, 0:1], T.pi[:, 2:3], 15, None, A.bitwise_and))
+    k_b = op("v", [k_pcol], lambda: ts(T.pi[:, 1:2], T.pi[:, 2:3], 4, None, A.logical_shift_right))
+    k_pf = op("v", [k_a, k_b], lambda: V.tensor_copy(T.pf[:, 0:2], T.pi[:, 0:2]))
+    k_rs16 = op("v", [k_r], lambda: V.memset(T.rs16[:, 0::16], 0.0))
+    k_colf = op("v", [k_pf], lambda: ts(T.pf[:, 2:3], T.pf[:, 0:1], 8.0, T.pf[:, 1:2], A.mult, A.add))
+    k_gkey = op("v", [k_pf], lambda: ts(T.pf[:, 3:4], T.pf[:, 1:2], float(gi << 19), None, A.add))
+    k_s = op("v", [k_pf, k_it16], lambda: ts(T.smat[:], T.it16[:], T.pf[:, 0:1], None, A.is_equal))
+    k_offe = op("v", [k_colf, k_it2], lambda: ts(T.offe[:], T.pi[:, 3:5], T.pf[:, 2:3], None, A.add))
+
+    if is_rank:
+        wait("p", tok_idx)
+        if is_sorter:
+            send([fl["S"]], T.lsf[:], T.lst[:], "lsf", off_mask)
+        send([me["Q"]], T.lst[:], T.lst[:], "lst", on_mask)
+        for h in range(NP):
+            c0 = 2048 * li + pw * h
+            piece = T.win[:, c0:c0 + pw]
+            wait("p", tok_map[h])
+            send([me["Q"]], piece, piece, "m%d%d" % (li, h), on_mask, "ms")
+            send([lanes[(li + k) % nl]["R"] for k in range(1, nl)], piece, piece, "m%d%d" % (li, h), on_mask, "ms")
+    else:
+        if is_sorter:
+            wait("p", ("lst", bits(on_mask)))
+            send([fl["S"]], T.lsf[:], T.lst[:], "lsf", off_mask)
+        for h in range(NP):
+            c0 = 2048 * li + pw * h
+            piece = T.win[:, c0:c0 + pw]
+            wait("p", ("m%d%d" % (li, h), bits(on_mask)))
+            send([lanes[(li + k) % nl]["Q"] for k in range(1, nl)], piece, piece, "m%d%d" % (li, h), on_mask)
+    if is_rank:
+        wait("s", ("ms", cnt["ms"]))
+        tok_tab = dma("s", "dtab", T.tw[:], T.tab[:])
+
+    far_proc = is_sorter
+    ls = T.lsf if far_proc else T.lst
+    if far_proc:
+        have = ("lsf", bits(off_mask))
+    elif is_rank:
+        have = tok_idx
+    else:
+        have = ("lst", bits(on_mask))
+    a = op("v", [have], lambda: ts(T.ti[:, 0:256], ls[:], 1, 7 | (1 << 19), A.logical_shift_right, A.bitwise_and))
+    b = op("v", [], lambda: ts(T.ti[:, 256:512], ls[:], 17, 7, A.logical_shift_right, A.bitwise_and))
+    c = op("v", [], lambda: ts(T.ti[:, 512:768], ls[:], 4, 1023, A.logical_shift_right, A.bitwise_and))
+    e = op("v", [k_offe], lambda: V.tensor_copy(T.ei[:], ls[:, 0:256].indirect(T.offe[:, 0:2])))
+    a = op("v", [a, k_gkey], lambda: ts(T.tf[:, 0:256], T.ti[:, 0:256], T.pf[:, 3:4], 16384.0, A.not_equal, A.mult))
+    b = op("v", [b], lambda: ts(T.tf[:, 256:512], T.ti[:, 256:512], 1024.0, None, A.mult))
+    e = op("v", [e], lambda: ts(T.em[:], T.ei[:], 1 | (7 << 14), None, A.bitwise_and))
+    c = op("v", [a, c], lambda: V.tensor_tensor(T.tf[:, 512:768], T.tf[:, 0:256], T.ti[:, 512:768], A.add))
+    d = op("v", [c, b], lambda: V.tensor_tensor(T.tf[:, 768:1024], T.tf[:, 512:768], T.tf[:, 256:512], A.add))
+    k_off1 = op("v", [d], lambda: ts(T.off1[:], T.tf[:, 768:1024], float(Z), None, A.min))
+    for t in range(16):
+        k_oh = op("v", [e], lambda: ts(T.oh[:, t::16], T.em[:], float((t >> 3) + ((t & 7) << 14)), None, A.is_equal))
+
+    if is_sorter or is_rank:
+        k_ones = op("v", [], lambda: V.memset(T.ones[:], 1.0))
+        k_rep = op("p", [k_ones], lambda: g.affine_select(T.rep[:], T.ones[:], [[-16, 8], [0, 8], [-1, 16]], A.is_equal,
+                                                          0.0, 0, 1))
+        if is_sorter:
+            k_neg = op("v", [], lambda: V.memset(T.neg[:], -1.0))
+            k_q = op("v", [], lambda: V.memset(T.rs32[:], 1.0))
+            k_rs32 = op("v", [k_q], lambda: V.memset(T.rs32[:, 0::32], 0.0))
+            k_it = op("p", [], lambda: g.iota(T.it128[:], [[1, 128]], 0, 0, allow_small_or_imprecise_dtypes=True))
+            k_base = op("p", [], lambda: g.iota(T.base[0:1, :], [[1024, 8], [0, 32]], 0, 0,
+                                                allow_small_or_imprecise_dtypes=True))
+            k_tri = op("p", [k_neg], lambda: g.affine_select(T.tri[:], T.neg[:], [[-1, 128]], A.is_ge, 0.0, 0, 1))
+        k_rep7 = op("v", [k_rep], lambda: ts(T.rep7[:], T.rep[:], 128.0, None, A.mult))
+
+    for i in range(nl):
+        for h in range(NP):
+            if is_rank and i == li:
+                wait("v", tok_map[h])
+            else:
+                wait("v", ("m%d%d" % (i, h), bits(on_mask)))
+    n0 = 0
+    pv = [T.pv0, T.pv1]
+    half = [None, None]
+    for n in (512, 1024, 1024, 1024, 512):
+        tg = op("v", [k_off1, k_z], lambda: V.tensor_copy(
+            T.gat[:, n0:n0 + n], T.win[:, 0:Z + 4].indirect(T.off1[:, n0 // 16:(n0 + n) // 16])))
+        for k in range(n0 // 128, (n0 + n) // 128):
+            half[k // 16] = op("t", [tg, k_s], lambda: g.tensor.matmul(
+                pv[k // 16][:, 16 * (k % 16):16 * (k % 16) + 16], T.gat[:, 128 * k:128 * k + 128], T.smat[:], True, True))
+        n0 += n
+    for h in range(2):
+        w = slice(256 * h, 256 * h + 256)
+        x = op("v", [half[h], k_oh], lambda: V.tensor_tensor(T.xm[:, w], pv[h][:, 0:256], T.oh[:, w], A.mult))
+        x = op("v", [x, k_rs16], lambda: V.tensor_tensor_scan(T.xs[:, w], T.rs16[:], T.xm[:, w], 0.0, A.mult, A.add))
+        k_res = op("v", [x], lambda: V.tensor_copy(T.res[:, 16 * h:16 * h + 16], T.xs[:, 256 * h + 15:256 * h + 256:16]))
+    wait("p", k_res)
+    if far_proc:
+        send([fl["S"]], T.rb[:], T.res[:], "rf", off_mask)
+    else:
+        send([me["S"]], T.ra[:], T.res[:], "rh", on_mask)
+
+    if is_sorter:
+        k_v = op("v", [("rh", bits(on_mask)), ("rf", bits(off_mask))],
+                 lambda: V.tensor_tensor(T.vi[:], T.ra[:], T.rb[:], A.add))
+        k_o = op("v", [k_v], lambda: ts(T.o2[:], T.vi[:], 13, None, A.logical_shift_right))
+        x0 = op("v", [], lambda: ts(T.ib[:, 0:32], T.vi[:], 7, 63, A.logical_shift_right, A.bitwise_and))
+        x1 = op("v", [], lambda: ts(T.ib[:, 32:64], T.vi[:], 127, None, A.bitwise_and))
+        for o in range(8):
+            k_m = op("v", [k_o], lambda: ts(T.msk[:, 32 * o:32 * o + 32], T.o2[:], float(o), None, A.is_equal))
+        k_sc = op("v", [k_m, k_rs32], lambda: V.tensor_tensor_scan(T.scn[:], T.rs32[:], T.msk[:], 0.0, A.mult, A.add))
+        k_f0 = op("v", [x0, x1], lambda: V.tensor_copy(T.fb[:, 0:64], T.ib[:, 0:64]))
+        op("t", [k_base, k_ones], lambda: g.tensor.matmul(T.prk[:, 0:256], T.ones[0:1, 0:128], T.base[0:1, :], True, False))
+        op("t", [k_m, k_tri], lambda: g.tensor.matmul(T.prk[:, 0:256], T.tri[:], T.msk[:], False, False))
+        k_rk = op("t", [k_sc], lambda: g.tensor.matmul(T.prk[:, 0:256], T.ones[:, 0:128], T.scn[:], False, True))
+        x = op("v", [k_rk], lambda: V.tensor_tensor(T.pm[:], T.prk[:, 0:256], T.msk[:], A.mult))
+        x = op("v", [x], lambda: V.tensor_tensor(T.ss[:, 0:128], T.pm[:, 0:128], T.pm[:, 128:256], A.add))
+        x = op("v", [x], lambda: V.tensor_tensor(T.ss[:, 128:192], T.ss[:, 0:64], T.ss[:, 64:128], A.add))
+        k_pos = op("v", [x], lambda: V.tensor_tensor(T.pos[:], T.ss[:, 128:160], T.ss[:, 160:192], A.add))
+        op("v", [k_pos], lambda: ts(T.ib[:, 64:96], T.pos[:], 6, None, A.logical_shift_right))
+        x = op("v", [], lambda: ts(T.ib[:, 96:128], T.pos[:], 63, None, A.bitwise_and))
+        k_f1 = op("v", [x], lambda: V.tensor_copy(T.fb[:, 64:128], T.ib[:, 64:128]))
+        for k in range(32):
+            lo = 128 * k
+            op("v", [k_f1, k_f0, k_it], lambda: ts(T.lhs[:, lo:lo + 128], T.it128[:], T.fb[:, 64 + k:65 + k], None,
+                                                   A.is_equal))
+            op("v", [], lambda: ts(T.rhs[:, lo:lo + 64], T.it128[:, 0:64], T.fb[:, 96 + k:97 + k], T.fb[:, k:k + 1],
+                                   A.is_equal, A.mult))
+            x = op("v", [], lambda: ts(T.rhs[:, lo + 64:lo + 128], T.it128[:, 0:64], T.fb[:, 96 + k:97 + k],
+                                       T.fb[:, 32 + k:33 + k], A.is_equal, A.mult))
+            k_l = op("t", [x], lambda: g.tensor.matmul(T.pl[:, 0:128], T.lhs[:, lo:lo + 128], T.rhs[:, lo:lo + 128],
+                                                       k == 0, k == 31))
+        slot = T.LL[:, 128 * myr:128 * myr + 128]
+        k_ll = op("v", [k_l], lambda: V.tensor_copy(slot, T.pl[:, 0:128]))
+        wait("p", k_ll)
+        send([flanes[(li + k) % nl]["R"] for k in range(nl)], slot, slot, "L%d" % myr, off_mask)
+        near = [lanes[(li + k) % nl]["R"] for k in range(nl)]
+        send([d for d in near if d != core], slot, slot, "L%d" % myr, on_mask)
+
+    def order_offsets():
+        x0 = op("v", [k_pos], lambda: ts(T.qi[:, 0:32], T.pos[:], 10, None, A.logical_shift_right))
+        x1 = op("v", [], lambda: ts(T.qi[:, 32:64], T.pos[:], 7, None, A.bitwise_and))
+        x2 = op("v", [], lambda: ts(T.qi[:, 64:96], T.pos[:], 3, 7, A.logical_shift_right, A.bitwise_and))
+        x3 = op("v", [], lambda: ts(T.qi[:, 96:128], T.pos[:], 6, 15, A.logical_shift_right, A.bitwise_and))
+        op("v", [x0], lambda: ts(T.qf[:, 0:32], T.qi[:, 0:32], 8.0, None, A.mult))
+        x = op("v", [x1], lambda: ts(T.qf[:, 32:64], T.qi[:, 32:64], 16.0, None, A.mult))
+        k_qb = op("v", [x, x2, x3], lambda: V.tensor_tensor(T.qb[:], T.qf[:], T.qi[:, 64:128], A.add))
+        for q in range(8):
+            w = slice(128 * q, 128 * q + 128)
+            op("t", [k_qb, k_rep7, k_res], lambda: g.tensor.matmul(T.pv0[:, 32 * q:32 * q + 32], T.rep7[:, w],
+                                                                   T.qb[:, 0:32], True, False))
+            x = op("t", [], lambda: g.tensor.matmul(T.pv0[:, 32 * q:32 * q + 32], T.rep[:, w], T.qb[:, 32:64], False, True))
+        for q in range(8):
+            y = op("v", [x], lambda: V.tensor_copy(T.off2[:, q::8], T.pv0[:, 32 * q:32 * q + 32]))
+        return y
+
+    def pieces(t):
+        return [(0, 512), (512, 1024)] if t == 0 else [(0, 1024)]
+
+    if is_sorter and not is_rank:
+        k_off2 = order_offsets()
+        wait("p", k_off2)
+        send([me["R"]], T.off2[:], T.off2[:], "off2", on_mask)
+        n = 0
+        for t in range(nl):
+            dst = flanes[(li + t) % nl]["R"]
+            for lo, hi in pieces(t):
+                wait("p", ("rl%d" % n, bits(on_mask)))
+                send([dst], T.land[:, 1024 * myr + lo:1024 * myr + hi], T.rly[:, 1024 * t + lo:1024 * t + hi],
+                     "d%d" % myr, off_mask)
+                n += 1
+
+    if is_rank:
+        near_mask = (on_mask & ~off_mask) if is_sorter else on_mask
+        items = []
+        for t in range(nl):
+            items.append(("f", t, far_r[(li + t) % nl]))
+            items.append(("n", t, near_r[(li + 1 + t) % nl]))
+        pr = [T.pr0, T.pr1, T.pr2, T.pr3]
+        copied = []
+        w = slice(128 * myr, 128 * myr + 128)
+        npc = 0
+        for j, (kind, t, r) in enumerate(items):
+            s_mask = off_mask if kind == "f" else on_mask
+            dep = k_ll if (r == myr and is_sorter) else ("L%d" % r, bits(s_mask))
+            back = copied[j - 4] if j >= 4 else None
+            op("t", [dep, back, k_rep7], lambda: g.tensor.matmul(pr[j % 4][:, 0:64], T.rep7[:, w],
+                                                                 T.LL[:, 128 * r:128 * r + 64], True, False))
+            x = op("t", [], lambda: g.tensor.matmul(pr[j % 4][:, 0:64], T.rep[:, w],
+                                                    T.LL[:, 128 * r + 64:128 * r + 128], False, True))
+            k_c = op("v", [x], lambda: V.tensor_copy(T.offr[:, 64 * r:64 * r + 64], pr[j % 4][:, 0:64]))
+            copied.append(k_c)
+            for lo, hi in (pieces(t) if kind == "f" else [(0, 1024)]):
+                if r == myr:
+                    out = T.land[:, 1024 * myr:1024 * myr + 1024]
+                else:
+                    out = T.og[:, 1024 * j + lo:1024 * j + hi]
+                off = T.offr[:, 64 * r + lo // 16:64 * r + hi // 16]
+                if kind == "f":
+                    k_g = op("v", [k_c, tok_tab], lambda: V.tensor_copy(out, T.tw[:, 0:8192].indirect(off)))
+                else:
+                    k_g = op("a", [k_c, tok_tab], lambda: S.activation(out, T.tw[:, 0:8192].indirect(off),
+                                                                       ActivationFunctionType.Copy))
+                if r == myr:
+                    k_own = k_g
+                    continue
+                wait("p", k_g)
+                dst = T.land[:, 1024 * myr + lo:1024 * myr + hi]
+                if kind == "n":
+                    send([cores[r]], dst, out, "d%d" % myr, near_mask)
+                elif is_sorter:
+                    send([cores[r]], dst, out, "d%d" % myr, off_mask)
+                else:
+                    send([me["Q"]], T.rly[:, 1024 * t + lo:1024 * t + hi], out, "rl%d" % npc, on_mask)
+                    npc += 1
+        if is_sorter:
+            k_off2 = order_offsets()
+        else:
+            k_off2 = ("off2", bits(on_mask))
+
+        last = [k_off2, k_own]
+        for i in range(nl):
+            if i != li:
+                other_sorter = lanes[i]["R"] == lanes[i]["S"]
+                last.append(("d%d" % near_r[i], bits(on_mask & ~off_mask) if other_sorter else bits(on_mask)))
+            last.append(("d%d" % far_r[i], bits(off_mask) * len(pieces((li - i) % nl))))
+        for k in range(2):
+            lo = 1024 * k
+            hi = 2048 + lo
+            x = op("v", last, lambda: V.tensor_copy(T.yb[:, lo:lo + 1024],
+                                                    T.land[:, 0:8192].indirect(T.off2[:, lo // 16:lo // 16 + 64])))
+            wait("s", x)
+            dma("s", "dy", T.y[:, lo:lo + 1024], T.yb[:, lo:lo + 1024])
+            x = op("a", last, lambda: S.activation(T.yb[:, hi:hi + 1024],
+                                                   T.land[:, 0:8192].indirect(T.off2[:, hi // 16:hi // 16 + 64]),
+                                                   ActivationFunctionType.Copy))
+            wait("s", x)
+            dma("s", "dy", T.y[:, hi:hi + 1024], T.yb[:, hi:hi + 1024])
+
+    for s in sorted(cnt):
+        if cnt[s]:
+            wait("p", (s, cnt[s]))
+    for s in sorted(dma_tot):
+        wait("p", (s, dma_tot[s]))

@@ -3,7 +3,10 @@ from concourse.mybir import AluOpType, ActivationFunctionType
 
 SIM = 112
 NP = 2
+CB = 10
 Z = 8192
+SEL = 24
+SPLIT = 22
 
 SCRATCH = {
     "lst": ("sbuf", [128, 256], "int32"),
@@ -14,7 +17,7 @@ SCRATCH = {
     "offe": ("sbuf", [128, 2], "uint16"),
     "it16": ("sbuf", [128, 16], "float32"),
     "smat": ("sbuf", [128, 16], "float32"),
-    "rs16": ("sbuf", [128, 256], "float32"),
+    "rs16": ("sbuf", [128, 512], "float32"),
     "ti": ("sbuf", [128, 768], "int32"),
     "tf": ("sbuf", [128, 1024], "float32"),
     "off1": ("sbuf", [128, 256], "uint16"),
@@ -39,6 +42,8 @@ SCRATCH = {
     "o2": ("sbuf", [128, 32], "int32"),
     "ib": ("sbuf", [128, 128], "int32"),
     "fb": ("sbuf", [128, 128], "float32"),
+    "nb": ("sbuf", [128, 128], "float32"),
+    "ab": ("sbuf", [128, 2304], "bfloat16"),
     "msk": ("sbuf", [128, 256], "bfloat16"),
     "scn": ("sbuf", [128, 256], "bfloat16"),
     "pm": ("sbuf", [128, 256], "float32"),
@@ -53,7 +58,7 @@ SCRATCH = {
     "off2": ("sbuf", [128, 256], "uint16"),
     "tw": ("sbuf", [128, 8192], "float32"),
     "offr": ("sbuf", [128, 512], "uint16"),
-    "og": ("sbuf", [128, 7168], "float32"),
+    "og": ("sbuf", [128, 8192], "float32"),
     "land": ("sbuf", [128, 8192], "float32"),
     "rly": ("sbuf", [128, 4096], "float32"),
     "yb": ("sbuf", [128, 4096], "float32"),
@@ -66,9 +71,10 @@ SCRATCH = {
     "pr2": ("psum", [128, 512], "float32"),
     "pr3": ("psum", [128, 512], "float32"),
 }
-SEMAPHORES = (["cv", "ct", "ca", "cp", "dix", "dm0", "dm1", "dtab", "dy", "lst", "lsf", "rh", "rf", "off2", "ls", "ms"]
+SEMAPHORES = (["cv", "ct", "ca", "cp", "dix", "dy", "dtab", "lst", "lsf", "rh", "rf", "off2", "ls", "ms"]
+              + ["dm%d" % k for k in range(NP)] + ["rl%d" % r for r in range(5)]
               + ["m%d%d" % (i, h) for i in range(4) for h in range(NP)]
-              + ["L%d" % r for r in range(8)] + ["d%d" % r for r in range(8)] + ["rl%d" % r for r in range(5)])
+              + ["L%d" % r for r in range(8)] + ["d%d" % r for r in range(8)])
 
 
 def _lanes(cores, chip, topo):
@@ -88,6 +94,7 @@ def _lanes(cores, chip, topo):
 
 def rank_program(g, core, T, topo):
     A = AluOpType
+    AF = ActivationFunctionType
     cores = list(T.cores)
     chips = []
     for c in cores:
@@ -111,6 +118,7 @@ def rank_program(g, core, T, topo):
     myr = cores.index(me["R"])
     on_mask = topo.mask(me["R"], me["Q"])
     off_mask = topo.mask(me["S"], fl["S"])
+    side_mask = on_mask & ~off_mask
 
     queues = {"v": g.vector, "t": g.tensor, "a": g.scalar, "p": g, "s": g.sync}
     cnt = {"cv": 0, "ct": 0, "ca": 0, "cp": 0, "ls": 0, "ms": 0}
@@ -164,23 +172,31 @@ def rank_program(g, core, T, topo):
 
     hw = 16384 // NP
     pw = 2048 // NP
+
+    def piece(h):
+        return T.win[:, 2048 * li + pw * h:2048 * li + pw * h + pw]
+
     if is_rank:
         for k in range(8):
             tok_idx = dma("s" if k % 2 == 0 else "a", "dix", T.lst[16 * k:16 * k + 16, :], T.idx[:])
-        tok_map = []
-        for h in range(NP):
-            c0 = 2048 * li + pw * h
-            tok_map.append(dma("s", "dm%d" % h, T.win[:, c0:c0 + pw], T.mp[:, hw * h:hw * h + hw]))
+        tok_map = [dma("s", "dm%d" % h, piece(h), T.mp[:, hw * h:hw * h + hw]) for h in range(NP)]
 
     k_pcol = op("p", [], lambda: g.iota(T.pi[:, 2:3], [[0, 1]], 0, 1))
     k_it2 = op("p", [], lambda: g.iota(T.pi[:, 3:5], [[128, 2]], 0, 0))
     k_it16 = op("p", [], lambda: g.iota(T.it16[:], [[1, 16]], 0, 0, allow_small_or_imprecise_dtypes=True))
     k_z = op("v", [], lambda: V.memset(T.win[:, Z:Z + 4], 0))
     k_r = op("v", [], lambda: V.memset(T.rs16[:], 1.0))
+    if is_sorter or is_rank:
+        k_ones = op("v", [], lambda: V.memset(T.ones[:], 1.0))
+    if is_sorter:
+        k_neg = op("v", [], lambda: V.memset(T.neg[:], -1.0))
+        k_q = op("v", [], lambda: V.memset(T.rs32[:], 1.0))
     k_a = op("v", [k_pcol], lambda: ts(T.pi[:, 0:1], T.pi[:, 2:3], 15, None, A.bitwise_and))
     k_b = op("v", [k_pcol], lambda: ts(T.pi[:, 1:2], T.pi[:, 2:3], 4, None, A.logical_shift_right))
     k_pf = op("v", [k_a, k_b], lambda: V.tensor_copy(T.pf[:, 0:2], T.pi[:, 0:2]))
     k_rs16 = op("v", [k_r], lambda: V.memset(T.rs16[:, 0::16], 0.0))
+    if is_sorter:
+        k_rs32 = op("v", [k_q], lambda: V.memset(T.rs32[:, 0::32], 0.0))
     k_colf = op("v", [k_pf], lambda: ts(T.pf[:, 2:3], T.pf[:, 0:1], 8.0, T.pf[:, 1:2], A.mult, A.add))
     k_gkey = op("v", [k_pf], lambda: ts(T.pf[:, 3:4], T.pf[:, 1:2], float(gi << 19), None, A.add))
     k_s = op("v", [k_pf, k_it16], lambda: ts(T.smat[:], T.it16[:], T.pf[:, 0:1], None, A.is_equal))
@@ -192,82 +208,78 @@ def rank_program(g, core, T, topo):
             send([fl["S"]], T.lsf[:], T.lst[:], "lsf", off_mask)
         send([me["Q"]], T.lst[:], T.lst[:], "lst", on_mask)
         for h in range(NP):
-            c0 = 2048 * li + pw * h
-            piece = T.win[:, c0:c0 + pw]
             wait("p", tok_map[h])
-            send([me["Q"]], piece, piece, "m%d%d" % (li, h), on_mask, "ms")
-            send([lanes[(li + k) % nl]["R"] for k in range(1, nl)], piece, piece, "m%d%d" % (li, h), on_mask, "ms")
+            send([me["Q"]], piece(h), piece(h), "m%d%d" % (li, h), on_mask, "ms")
+        part = T.win[:, 2048 * li:2048 * li + 2048]
+        send([lanes[(li + k) % nl]["R"] for k in range(1, nl)], part, part, "m%d0" % li, on_mask, "ms")
     else:
         if is_sorter:
             wait("p", ("lst", bits(on_mask)))
             send([fl["S"]], T.lsf[:], T.lst[:], "lsf", off_mask)
         for h in range(NP):
-            c0 = 2048 * li + pw * h
-            piece = T.win[:, c0:c0 + pw]
             wait("p", ("m%d%d" % (li, h), bits(on_mask)))
-            send([lanes[(li + k) % nl]["Q"] for k in range(1, nl)], piece, piece, "m%d%d" % (li, h), on_mask)
+            send([lanes[(li + k) % nl]["Q"] for k in range(1, nl)], piece(h), piece(h), "m%d%d" % (li, h), on_mask)
     if is_rank:
         wait("s", ("ms", cnt["ms"]))
         tok_tab = dma("s", "dtab", T.tw[:], T.tab[:])
 
-    far_proc = is_sorter
-    ls = T.lsf if far_proc else T.lst
-    if far_proc:
+    if is_sorter or is_rank:
+        k_rep = op("p", [k_ones], lambda: g.affine_select(T.rep[:], T.ones[:], [[-16, 8], [0, 8], [-1, 16]], A.is_equal,
+                                                          0.0, 0, 1))
+    if is_sorter:
+        k_it = op("p", [], lambda: g.iota(T.it128[:], [[1, 128]], 0, 0, allow_small_or_imprecise_dtypes=True))
+        k_base = op("p", [], lambda: g.iota(T.base[0:1, :], [[1024, 8], [0, 32]], 0, 0,
+                                            allow_small_or_imprecise_dtypes=True))
+        k_tri = op("p", [k_neg], lambda: g.affine_select(T.tri[:], T.neg[:], [[-1, 128]], A.is_ge, 0.0, 0, 1))
+
+    ls = T.lsf if is_sorter else T.lst
+    if is_sorter:
         have = ("lsf", bits(off_mask))
     elif is_rank:
         have = tok_idx
     else:
         have = ("lst", bits(on_mask))
     a = op("v", [have], lambda: ts(T.ti[:, 0:256], ls[:], 1, 7 | (1 << 19), A.logical_shift_right, A.bitwise_and))
-    b = op("v", [], lambda: ts(T.ti[:, 256:512], ls[:], 17, 7, A.logical_shift_right, A.bitwise_and))
-    c = op("v", [], lambda: ts(T.ti[:, 512:768], ls[:], 4, 1023, A.logical_shift_right, A.bitwise_and))
+    b = op("v", [], lambda: ts(T.ti[:, 256:512], ls[:], 7 + CB, 4 * NP - 1, A.logical_shift_right, A.bitwise_and))
+    c = op("v", [], lambda: ts(T.ti[:, 512:768], ls[:], 4, (1 << CB) - 1, A.logical_shift_right, A.bitwise_and))
     e = op("v", [k_offe], lambda: V.tensor_copy(T.ei[:], ls[:, 0:256].indirect(T.offe[:, 0:2])))
     a = op("v", [a, k_gkey], lambda: ts(T.tf[:, 0:256], T.ti[:, 0:256], T.pf[:, 3:4], 16384.0, A.not_equal, A.mult))
-    b = op("v", [b], lambda: ts(T.tf[:, 256:512], T.ti[:, 256:512], 1024.0, None, A.mult))
-    e = op("v", [e], lambda: ts(T.em[:], T.ei[:], 1 | (7 << 14), None, A.bitwise_and))
+    b = op("v", [b], lambda: ts(T.tf[:, 256:512], T.ti[:, 256:512], float(1 << CB), None, A.mult))
+    e = op("v", [e], lambda: ts(T.em[:], T.ei[:], 1 | (7 << (4 + CB)), None, A.bitwise_and))
     c = op("v", [a, c], lambda: V.tensor_tensor(T.tf[:, 512:768], T.tf[:, 0:256], T.ti[:, 512:768], A.add))
     d = op("v", [c, b], lambda: V.tensor_tensor(T.tf[:, 768:1024], T.tf[:, 512:768], T.tf[:, 256:512], A.add))
     k_off1 = op("v", [d], lambda: ts(T.off1[:], T.tf[:, 768:1024], float(Z), None, A.min))
     for t in range(16):
-        k_oh = op("v", [e], lambda: ts(T.oh[:, t::16], T.em[:], float((t >> 3) + ((t & 7) << 14)), None, A.is_equal))
-
+        k_oh = op("v", [e], lambda: ts(T.oh[:, t::16], T.em[:], float((t >> 3) + ((t & 7) << (4 + CB))), None, A.is_equal))
     if is_sorter or is_rank:
-        k_ones = op("v", [], lambda: V.memset(T.ones[:], 1.0))
-        k_rep = op("p", [k_ones], lambda: g.affine_select(T.rep[:], T.ones[:], [[-16, 8], [0, 8], [-1, 16]], A.is_equal,
-                                                          0.0, 0, 1))
-        if is_sorter:
-            k_neg = op("v", [], lambda: V.memset(T.neg[:], -1.0))
-            k_q = op("v", [], lambda: V.memset(T.rs32[:], 1.0))
-            k_rs32 = op("v", [k_q], lambda: V.memset(T.rs32[:, 0::32], 0.0))
-            k_it = op("p", [], lambda: g.iota(T.it128[:], [[1, 128]], 0, 0, allow_small_or_imprecise_dtypes=True))
-            k_base = op("p", [], lambda: g.iota(T.base[0:1, :], [[1024, 8], [0, 32]], 0, 0,
-                                                allow_small_or_imprecise_dtypes=True))
-            k_tri = op("p", [k_neg], lambda: g.affine_select(T.tri[:], T.neg[:], [[-1, 128]], A.is_ge, 0.0, 0, 1))
         k_rep7 = op("v", [k_rep], lambda: ts(T.rep7[:], T.rep[:], 128.0, None, A.mult))
 
     for i in range(nl):
         for h in range(NP):
             if is_rank and i == li:
                 wait("v", tok_map[h])
-            else:
+            elif not is_rank or h == 0:
                 wait("v", ("m%d%d" % (i, h), bits(on_mask)))
     n0 = 0
     pv = [T.pv0, T.pv1]
     half = [None, None]
-    for n in (512, 1024, 1024, 1024, 512):
+    for n in (256, 768, 1024, 1024, 1024):
         tg = op("v", [k_off1, k_z], lambda: V.tensor_copy(
             T.gat[:, n0:n0 + n], T.win[:, 0:Z + 4].indirect(T.off1[:, n0 // 16:(n0 + n) // 16])))
         for k in range(n0 // 128, (n0 + n) // 128):
-            half[k // 16] = op("t", [tg, k_s], lambda: g.tensor.matmul(
-                pv[k // 16][:, 16 * (k % 16):16 * (k % 16) + 16], T.gat[:, 128 * k:128 * k + 128], T.smat[:], True, True))
+            c0 = 16 * (k % SEL)
+            half[k // SEL] = op("t", [tg, k_s], lambda: g.tensor.matmul(
+                pv[k // SEL][:, c0:c0 + 16], T.gat[:, 128 * k:128 * k + 128], T.smat[:], True, True))
         n0 += n
     for h in range(2):
-        w = slice(256 * h, 256 * h + 256)
-        x = op("v", [half[h], k_oh], lambda: V.tensor_tensor(T.xm[:, w], pv[h][:, 0:256], T.oh[:, w], A.mult))
-        x = op("v", [x, k_rs16], lambda: V.tensor_tensor_scan(T.xs[:, w], T.rs16[:], T.xm[:, w], 0.0, A.mult, A.add))
-        k_res = op("v", [x], lambda: V.tensor_copy(T.res[:, 16 * h:16 * h + 16], T.xs[:, 256 * h + 15:256 * h + 256:16]))
+        w0, w1 = (0, 16 * SEL) if h == 0 else (16 * SEL, 512)
+        n = w1 - w0
+        x = op("v", [half[h], k_oh], lambda: V.tensor_tensor(T.xm[:, w0:w1], pv[h][:, 0:n], T.oh[:, w0:w1], A.mult))
+        x = op("v", [x, k_rs16], lambda: V.tensor_tensor_scan(T.xs[:, w0:w1], T.rs16[:, 0:n], T.xm[:, w0:w1], 0.0, A.mult,
+                                                              A.add))
+        k_res = op("v", [x], lambda: V.tensor_copy(T.res[:, w0 // 16:w1 // 16], T.xs[:, w0 + 15:w1:16]))
     wait("p", k_res)
-    if far_proc:
+    if is_sorter:
         send([fl["S"]], T.rb[:], T.res[:], "rf", off_mask)
     else:
         send([me["S"]], T.ra[:], T.res[:], "rh", on_mask)
@@ -276,38 +288,57 @@ def rank_program(g, core, T, topo):
         k_v = op("v", [("rh", bits(on_mask)), ("rf", bits(off_mask))],
                  lambda: V.tensor_tensor(T.vi[:], T.ra[:], T.rb[:], A.add))
         k_o = op("v", [k_v], lambda: ts(T.o2[:], T.vi[:], 13, None, A.logical_shift_right))
-        x0 = op("v", [], lambda: ts(T.ib[:, 0:32], T.vi[:], 7, 63, A.logical_shift_right, A.bitwise_and))
-        x1 = op("v", [], lambda: ts(T.ib[:, 32:64], T.vi[:], 127, None, A.bitwise_and))
         for o in range(8):
             k_m = op("v", [k_o], lambda: ts(T.msk[:, 32 * o:32 * o + 32], T.o2[:], float(o), None, A.is_equal))
         k_sc = op("v", [k_m, k_rs32], lambda: V.tensor_tensor_scan(T.scn[:], T.rs32[:], T.msk[:], 0.0, A.mult, A.add))
+        x0 = op("v", [], lambda: ts(T.ib[:, 0:32], T.vi[:], 7, 63, A.logical_shift_right, A.bitwise_and))
+        x1 = op("v", [], lambda: ts(T.ib[:, 32:64], T.vi[:], 127, None, A.bitwise_and))
         k_f0 = op("v", [x0, x1], lambda: V.tensor_copy(T.fb[:, 0:64], T.ib[:, 0:64]))
         op("t", [k_base, k_ones], lambda: g.tensor.matmul(T.prk[:, 0:256], T.ones[0:1, 0:128], T.base[0:1, :], True, False))
         op("t", [k_m, k_tri], lambda: g.tensor.matmul(T.prk[:, 0:256], T.tri[:], T.msk[:], False, False))
         k_rk = op("t", [k_sc], lambda: g.tensor.matmul(T.prk[:, 0:256], T.ones[:, 0:128], T.scn[:], False, True))
         x = op("v", [k_rk], lambda: V.tensor_tensor(T.pm[:], T.prk[:, 0:256], T.msk[:], A.mult))
         x = op("v", [x], lambda: V.tensor_tensor(T.ss[:, 0:128], T.pm[:, 0:128], T.pm[:, 128:256], A.add))
+        k_n0 = op("v", [k_f0], lambda: ts(T.nb[:, 0:64], T.fb[:, 0:64], -1.0, None, A.mult))
         x = op("v", [x], lambda: V.tensor_tensor(T.ss[:, 128:192], T.ss[:, 0:64], T.ss[:, 64:128], A.add))
         k_pos = op("v", [x], lambda: V.tensor_tensor(T.pos[:], T.ss[:, 128:160], T.ss[:, 160:192], A.add))
         op("v", [k_pos], lambda: ts(T.ib[:, 64:96], T.pos[:], 6, None, A.logical_shift_right))
         x = op("v", [], lambda: ts(T.ib[:, 96:128], T.pos[:], 63, None, A.bitwise_and))
         k_f1 = op("v", [x], lambda: V.tensor_copy(T.fb[:, 64:128], T.ib[:, 64:128]))
+        k_n1 = op("v", [k_f1], lambda: ts(T.nb[:, 64:128], T.fb[:, 64:128], -1.0, None, A.mult))
+        for k in range(SPLIT, 32):
+            w = 192 * (k - SPLIT)
+            op("a", [k_n1, k_n0, k_it], lambda: S.activation(T.ab[:, w:w + 128], T.it128[:], AF.Abs,
+                                                             bias=T.nb[:, 64 + k:65 + k]))
+            k_ab = op("a", [], lambda: S.activation(T.ab[:, w + 128:w + 192], T.it128[:, 0:64], AF.Abs,
+                                                    bias=T.nb[:, 96 + k:97 + k]))
+        done = []
+        for k in range(SPLIT, 32):
+            w, lo = 192 * (k - SPLIT), 128 * k
+            op("a", [k_ab], lambda: S.activation(T.lhs[:, lo:lo + 128], T.ab[:, w:w + 128], AF.Relu, bias=1.0, scale=-1.0))
+            op("a", [], lambda: S.activation(T.rhs[:, lo:lo + 64], T.ab[:, w + 128:w + 192], AF.Relu,
+                                             bias=T.fb[:, k:k + 1], scale=T.nb[:, k:k + 1]))
+            done.append(op("a", [], lambda: S.activation(T.rhs[:, lo + 64:lo + 128], T.ab[:, w + 128:w + 192], AF.Relu,
+                                                         bias=T.fb[:, 32 + k:33 + k], scale=T.nb[:, 32 + k:33 + k])))
         for k in range(32):
             lo = 128 * k
-            op("v", [k_f1, k_f0, k_it], lambda: ts(T.lhs[:, lo:lo + 128], T.it128[:], T.fb[:, 64 + k:65 + k], None,
-                                                   A.is_equal))
-            op("v", [], lambda: ts(T.rhs[:, lo:lo + 64], T.it128[:, 0:64], T.fb[:, 96 + k:97 + k], T.fb[:, k:k + 1],
-                                   A.is_equal, A.mult))
-            x = op("v", [], lambda: ts(T.rhs[:, lo + 64:lo + 128], T.it128[:, 0:64], T.fb[:, 96 + k:97 + k],
-                                       T.fb[:, 32 + k:33 + k], A.is_equal, A.mult))
+            if k < SPLIT:
+                op("v", [k_f1, k_f0, k_it], lambda: ts(T.lhs[:, lo:lo + 128], T.it128[:], T.fb[:, 64 + k:65 + k], None,
+                                                       A.is_equal))
+                op("v", [], lambda: ts(T.rhs[:, lo:lo + 64], T.it128[:, 0:64], T.fb[:, 96 + k:97 + k], T.fb[:, k:k + 1],
+                                       A.is_equal, A.mult))
+                x = op("v", [], lambda: ts(T.rhs[:, lo + 64:lo + 128], T.it128[:, 0:64], T.fb[:, 96 + k:97 + k],
+                                           T.fb[:, 32 + k:33 + k], A.is_equal, A.mult))
+            else:
+                x = done[k - SPLIT]
             k_l = op("t", [x], lambda: g.tensor.matmul(T.pl[:, 0:128], T.lhs[:, lo:lo + 128], T.rhs[:, lo:lo + 128],
                                                        k == 0, k == 31))
         slot = T.LL[:, 128 * myr:128 * myr + 128]
         k_ll = op("v", [k_l], lambda: V.tensor_copy(slot, T.pl[:, 0:128]))
         wait("p", k_ll)
-        send([flanes[(li + k) % nl]["R"] for k in range(nl)], slot, slot, "L%d" % myr, off_mask)
-        near = [lanes[(li + k) % nl]["R"] for k in range(nl)]
-        send([d for d in near if d != core], slot, slot, "L%d" % myr, on_mask)
+        send([flanes[(li - k) % nl]["R"] for k in range(nl)], slot, slot, "L%d" % myr, off_mask)
+        near = [lanes[(li - 1 - k) % nl]["R"] for k in range(nl)]
+        send([d for d in near if d != core], slot, slot, "L%d" % myr, side_mask)
 
     def order_offsets():
         x0 = op("v", [k_pos], lambda: ts(T.qi[:, 0:32], T.pos[:], 10, None, A.logical_shift_right))
@@ -332,82 +363,98 @@ def rank_program(g, core, T, topo):
     if is_sorter and not is_rank:
         k_off2 = order_offsets()
         wait("p", k_off2)
-        send([me["R"]], T.off2[:], T.off2[:], "off2", on_mask)
+        send([me["R"]], T.off2[:], T.off2[:], "off2", side_mask)
         n = 0
         for t in range(nl):
-            dst = flanes[(li + t) % nl]["R"]
             for lo, hi in pieces(t):
                 wait("p", ("rl%d" % n, bits(on_mask)))
-                send([dst], T.land[:, 1024 * myr + lo:1024 * myr + hi], T.rly[:, 1024 * t + lo:1024 * t + hi],
-                     "d%d" % myr, off_mask)
+                send([flanes[(li + t) % nl]["R"]], T.land[:, 1024 * myr + lo:1024 * myr + hi],
+                     T.rly[:, 1024 * t + lo:1024 * t + hi], "d%d" % myr, off_mask)
                 n += 1
 
     if is_rank:
-        near_mask = (on_mask & ~off_mask) if is_sorter else on_mask
-        items = []
-        for t in range(nl):
-            items.append(("f", t, far_r[(li + t) % nl]))
-            items.append(("n", t, near_r[(li + 1 + t) % nl]))
+        items = [("f", t, far_r[(li + t) % nl]) for t in range(nl)]
+        items += [("n", t, near_r[(li + 1 + t) % nl]) for t in range(nl)]
         pr = [T.pr0, T.pr1, T.pr2, T.pr3]
-        copied = []
         w = slice(128 * myr, 128 * myr + 128)
-        npc = 0
-        for j, (kind, t, r) in enumerate(items):
-            s_mask = off_mask if kind == "f" else on_mask
-            dep = k_ll if (r == myr and is_sorter) else ("L%d" % r, bits(s_mask))
-            back = copied[j - 4] if j >= 4 else None
-            op("t", [dep, back, k_rep7], lambda: g.tensor.matmul(pr[j % 4][:, 0:64], T.rep7[:, w],
-                                                                 T.LL[:, 128 * r:128 * r + 64], True, False))
+        back, tok = {}, {}
+
+        def spread(j):
+            kind, t, r = items[j]
+            dep = k_ll if (r == myr and is_sorter) else ("L%d" % r, bits(off_mask if kind == "f" else side_mask))
+            op("t", [dep, back.get(j - 4), k_rep7], lambda: g.tensor.matmul(
+                pr[j % 4][:, 0:64], T.rep7[:, w], T.LL[:, 128 * r:128 * r + 64], True, False))
             x = op("t", [], lambda: g.tensor.matmul(pr[j % 4][:, 0:64], T.rep[:, w],
                                                     T.LL[:, 128 * r + 64:128 * r + 128], False, True))
-            k_c = op("v", [x], lambda: V.tensor_copy(T.offr[:, 64 * r:64 * r + 64], pr[j % 4][:, 0:64]))
-            copied.append(k_c)
-            for lo, hi in (pieces(t) if kind == "f" else [(0, 1024)]):
-                if r == myr:
-                    out = T.land[:, 1024 * myr:1024 * myr + 1024]
-                else:
-                    out = T.og[:, 1024 * j + lo:1024 * j + hi]
-                off = T.offr[:, 64 * r + lo // 16:64 * r + hi // 16]
-                if kind == "f":
-                    k_g = op("v", [k_c, tok_tab], lambda: V.tensor_copy(out, T.tw[:, 0:8192].indirect(off)))
-                else:
-                    k_g = op("a", [k_c, tok_tab], lambda: S.activation(out, T.tw[:, 0:8192].indirect(off),
-                                                                       ActivationFunctionType.Copy))
-                if r == myr:
-                    k_own = k_g
-                    continue
-                wait("p", k_g)
-                dst = T.land[:, 1024 * myr + lo:1024 * myr + hi]
-                if kind == "n":
-                    send([cores[r]], dst, out, "d%d" % myr, near_mask)
-                elif is_sorter:
-                    send([cores[r]], dst, out, "d%d" % myr, off_mask)
-                else:
-                    send([me["Q"]], T.rly[:, 1024 * t + lo:1024 * t + hi], out, "rl%d" % npc, on_mask)
-                    npc += 1
-        if is_sorter:
-            k_off2 = order_offsets()
-        else:
-            k_off2 = ("off2", bits(on_mask))
+            back[j] = op("v", [x], lambda: V.tensor_copy(T.offr[:, 64 * r:64 * r + 64], pr[j % 4][:, 0:64]))
 
+        def gather(q, j, lo=0, hi=1024):
+            kind, t, r = items[j]
+            out = T.land[:, 1024 * myr:1024 * myr + 1024] if r == myr else T.og[:, 1024 * j + lo:1024 * j + hi]
+            off = T.offr[:, 64 * r + lo // 16:64 * r + hi // 16]
+            if q == "v":
+                tok[(j, lo)] = op("v", [back[j], tok_tab], lambda: V.tensor_copy(out, T.tw[:, 0:8192].indirect(off)))
+            else:
+                tok[(j, lo)] = op("a", [back[j], tok_tab], lambda: S.activation(out, T.tw[:, 0:8192].indirect(off), AF.Copy))
+
+        npc = [0]
+
+        def ship(j, lo=0, hi=1024):
+            kind, t, r = items[j]
+            wait("p", tok[(j, lo)])
+            src, dst = T.og[:, 1024 * j + lo:1024 * j + hi], T.land[:, 1024 * myr + lo:1024 * myr + hi]
+            if kind == "n":
+                send([cores[r]], dst, src, "d%d" % myr, side_mask if is_sorter else on_mask)
+            elif is_sorter:
+                send([cores[r]], dst, src, "d%d" % myr, off_mask)
+            else:
+                send([me["Q"]], T.rly[:, 1024 * t + lo:1024 * t + hi], src, "rl%d" % npc[0], on_mask)
+                npc[0] += 1
+
+        spread(0)
+        gather("v", 0, 0, 512)
+        spread(1)
+        gather("v", 0, 512, 1024)
+        gather("a", 1)
+        spread(2)
+        spread(3)
+        gather("v", 2)
+        gather("a", 3)
+        ship(0, 0, 512)
+        ship(0, 512, 1024)
+        ship(1)
+        ship(2)
+        ship(3)
+        spread(4)
+        spread(5)
+        gather("v", 4)
+        gather("a", 5)
+        spread(6)
+        spread(7)
+        gather("v", 6)
+        gather("a", 7)
+        for j in range(4, 7):
+            ship(j)
+        k_own = tok[(7, 0)]
+
+    if is_rank:
+        k_off2 = order_offsets() if is_sorter else ("off2", bits(side_mask))
         last = [k_off2, k_own]
         for i in range(nl):
             if i != li:
-                other_sorter = lanes[i]["R"] == lanes[i]["S"]
-                last.append(("d%d" % near_r[i], bits(on_mask & ~off_mask) if other_sorter else bits(on_mask)))
+                has_port = lanes[i]["R"] == lanes[i]["S"]
+                last.append(("d%d" % near_r[i], bits(side_mask) if has_port else bits(on_mask)))
             last.append(("d%d" % far_r[i], bits(off_mask) * len(pieces((li - i) % nl))))
-        for k in range(2):
-            lo = 1024 * k
+        for lo, n in ((0, 512), (512, 512), (1024, 1024)):
             hi = 2048 + lo
-            x = op("v", last, lambda: V.tensor_copy(T.yb[:, lo:lo + 1024],
-                                                    T.land[:, 0:8192].indirect(T.off2[:, lo // 16:lo // 16 + 64])))
+            x = op("v", last, lambda: V.tensor_copy(T.yb[:, lo:lo + n],
+                                                    T.land[:, 0:8192].indirect(T.off2[:, lo // 16:(lo + n) // 16])))
             wait("s", x)
-            dma("s", "dy", T.y[:, lo:lo + 1024], T.yb[:, lo:lo + 1024])
-            x = op("a", last, lambda: S.activation(T.yb[:, hi:hi + 1024],
-                                                   T.land[:, 0:8192].indirect(T.off2[:, hi // 16:hi // 16 + 64]),
-                                                   ActivationFunctionType.Copy))
+            dma("s", "dy", T.y[:, lo:lo + n], T.yb[:, lo:lo + n])
+            x = op("a", last, lambda: S.activation(T.yb[:, hi:hi + n],
+                                                   T.land[:, 0:8192].indirect(T.off2[:, hi // 16:(hi + n) // 16]), AF.Copy))
             wait("s", x)
-            dma("s", "dy", T.y[:, hi:hi + 1024], T.yb[:, hi:hi + 1024])
+            dma("s", "dy", T.y[:, hi:hi + n], T.yb[:, hi:hi + n])
 
     for s in sorted(cnt):
         if cnt[s]:

@@ -6,12 +6,18 @@ NP = 2
 CB = 10
 Z = 8192
 SEL = 24
-SPLIT = 22
+SPLIT = 20
+HT = 4096
+PORTLESS = "xqxqqxqx"
+PORT = "dkdddddd"
+NEAR_PORTLESS = "sos"
+NEAR_PORT = "sss"
 
 SCRATCH = {
     "lst": ("sbuf", [128, 256], "int32"),
     "lsf": ("sbuf", [128, 256], "int32"),
-    "win": ("sbuf", [128, 8196], "int32"),
+    "mi": ("sbuf", [128, 2048], "int32"),
+    "win": ("sbuf", [128, 8196], "float32"),
     "pi": ("sbuf", [128, 5], "int32"),
     "pf": ("sbuf", [128, 4], "float32"),
     "offe": ("sbuf", [128, 2], "uint16"),
@@ -24,34 +30,36 @@ SCRATCH = {
     "ei": ("sbuf", [128, 32], "int32"),
     "em": ("sbuf", [128, 32], "int32"),
     "oh": ("sbuf", [128, 512], "float32"),
-    "gat": ("sbuf", [128, 4096], "float32"),
     "xm": ("sbuf", [128, 512], "float32"),
     "xs": ("sbuf", [128, 512], "float32"),
     "res": ("sbuf", [128, 32], "float32"),
     "ra": ("sbuf", [128, 32], "float32"),
     "rb": ("sbuf", [128, 32], "float32"),
-    "it128": ("sbuf", [128, 128], "bfloat16"),
+    "ith": ("sbuf", [128, 128], "float32"),
+    "onef": ("sbuf", [128, 128], "float32"),
     "ones": ("sbuf", [128, 1024], "bfloat16"),
     "neg": ("sbuf", [128, 128], "bfloat16"),
     "tri": ("sbuf", [128, 128], "bfloat16"),
-    "base": ("sbuf", [1, 256], "bfloat16"),
-    "rs32": ("sbuf", [128, 256], "bfloat16"),
+    "base": ("sbuf", [1, 128], "bfloat16"),
+    "rs32": ("sbuf", [128, 128], "bfloat16"),
     "rep": ("sbuf", [128, 1024], "bfloat16"),
     "rep7": ("sbuf", [128, 1024], "bfloat16"),
+    "repf": ("sbuf", [128, 128], "float32"),
     "vi": ("sbuf", [128, 32], "int32"),
     "o2": ("sbuf", [128, 32], "int32"),
-    "ib": ("sbuf", [128, 128], "int32"),
-    "fb": ("sbuf", [128, 128], "float32"),
-    "nb": ("sbuf", [128, 128], "float32"),
-    "ab": ("sbuf", [128, 2304], "bfloat16"),
-    "msk": ("sbuf", [128, 256], "bfloat16"),
-    "scn": ("sbuf", [128, 256], "bfloat16"),
-    "pm": ("sbuf", [128, 256], "float32"),
-    "ss": ("sbuf", [128, 192], "float32"),
+    "ib": ("sbuf", [128, 96], "int32"),
+    "fb": ("sbuf", [128, 96], "float32"),
+    "nb": ("sbuf", [128, 96], "float32"),
+    "ab": ("sbuf", [128, 1536], "float32"),
+    "msk": ("sbuf", [128, 128], "bfloat16"),
+    "scn": ("sbuf", [128, 128], "bfloat16"),
+    "pm": ("sbuf", [128, 192], "float32"),
     "pos": ("sbuf", [128, 32], "int32"),
-    "lhs": ("sbuf", [128, 4096], "bfloat16"),
-    "rhs": ("sbuf", [128, 4096], "bfloat16"),
-    "LL": ("sbuf", [128, 1024], "bfloat16"),
+    "pz": ("sbuf", [128, 96], "int32"),
+    "lhs": ("sbuf", [128, 2048], "float32"),
+    "rhs": ("sbuf", [128, 2048], "float32"),
+    "LS": ("sbuf", [128, 64], "float32"),
+    "LL": ("sbuf", [128, 512], "float32"),
     "qi": ("sbuf", [128, 128], "int32"),
     "qf": ("sbuf", [128, 64], "float32"),
     "qb": ("sbuf", [128, 64], "bfloat16"),
@@ -71,9 +79,10 @@ SCRATCH = {
     "pr2": ("psum", [128, 512], "float32"),
     "pr3": ("psum", [128, 512], "float32"),
 }
-SEMAPHORES = (["cv", "ct", "ca", "cp", "dix", "dy", "dtab", "lst", "lsf", "rh", "rf", "off2", "ls", "ms"]
-              + ["dm%d" % k for k in range(NP)] + ["rl%d" % r for r in range(5)]
+SEMAPHORES = (["cv", "ct", "ca", "cp", "dix", "dy", "dtab", "lst", "lsf", "rh", "rf", "off2", "ph", "ls", "ms", "as"]
+              + ["dm%d" % k for k in range(NP)]
               + ["m%d%d" % (i, h) for i in range(4) for h in range(NP)]
+              + ["rl%d" % r for r in range(8)] + ["rk%d" % r for r in range(8)] + ["rx%d" % r for r in range(8)]
               + ["L%d" % r for r in range(8)] + ["d%d" % r for r in range(8)])
 
 
@@ -92,6 +101,25 @@ def _lanes(cores, chip, topo):
     return out
 
 
+def _relays(cores, chips, gi, lanes, topo):
+    out, used = {}, []
+    far = [c for c in cores if topo.chip(c) == chips[1 - gi]]
+    for li, l in enumerate(lanes):
+        if l["R"] == l["S"]:
+            continue
+        best = None
+        for x in range(SIM - 1, -1, -1):
+            cx = topo.chip(x)
+            if cx in chips or not topo.same_plane(cx, chips[gi]) or not all(topo.may_write(x, d) for d in far):
+                continue
+            key = ([topo.die(u) for u in used].count(topo.die(x)), [topo.chip(u) for u in used].count(cx))
+            if best is None or key < best[0]:
+                best = (key, x)
+        out[li] = best[1]
+        used.append(best[1])
+    return out
+
+
 def rank_program(g, core, T, topo):
     A = AluOpType
     AF = ActivationFunctionType
@@ -100,15 +128,20 @@ def rank_program(g, core, T, topo):
     for c in cores:
         if topo.chip(c) not in chips:
             chips.append(topo.chip(c))
-    if topo.chip(core) not in chips:
+    gi = li = None
+    for k in range(2):
+        ln = _lanes(cores, chips[k], topo)
+        rx = _relays(cores, chips, k, ln, topo)
+        for i in range(len(ln)):
+            if core in (ln[i]["R"], ln[i]["Q"], rx.get(i)):
+                gi, li = k, i
+    if gi is None:
         return
-    gi = chips.index(topo.chip(core))
     lanes = _lanes(cores, chips[gi], topo)
     flanes = _lanes(cores, chips[1 - gi], topo)
-    mine = [i for i in range(len(lanes)) if core in (lanes[i]["R"], lanes[i]["Q"])]
-    if not mine:
-        return
-    li = mine[0]
+    relay = _relays(cores, chips, gi, lanes, topo)
+    portless = [i for i in range(len(lanes)) if i in relay]
+    ported = [i for i in range(len(lanes)) if i not in relay]
     me, fl = lanes[li], flanes[li]
     nl = len(lanes)
     is_rank = core == me["R"]
@@ -116,12 +149,13 @@ def rank_program(g, core, T, topo):
     near_r = [cores.index(l["R"]) for l in lanes]
     far_r = [cores.index(l["R"]) for l in flanes]
     myr = cores.index(me["R"])
+    half_r = far_r if is_sorter else near_r
     on_mask = topo.mask(me["R"], me["Q"])
     off_mask = topo.mask(me["S"], fl["S"])
     side_mask = on_mask & ~off_mask
 
     queues = {"v": g.vector, "t": g.tensor, "a": g.scalar, "p": g, "s": g.sync}
-    cnt = {"cv": 0, "ct": 0, "ca": 0, "cp": 0, "ls": 0, "ms": 0}
+    cnt = {"cv": 0, "ct": 0, "ca": 0, "cp": 0, "ls": 0, "ms": 0, "as": 0}
     seen = {}
 
     def bits(m):
@@ -156,6 +190,27 @@ def rank_program(g, core, T, topo):
                                                   srcs=[src], dsts=[out] * len(dsts))], local_sem=T.sem[lsem])
         cnt[lsem] += bits(mask)
 
+    halves = [(way, n // 2, n % 2) for n, way in enumerate(PORT if li in ported else PORTLESS)]
+
+    def spot(way, n):
+        return [m for m in range(8) if halves[m][0] == way].index(n)
+
+    def forward(src, lane, t, hh, sem, mask):
+        r = cores.index(lanes[lane]["R"])
+        wait("p", (sem, bits(mask)))
+        send([flanes[(lane + t) % nl]["R"]], T.land[:, 1024 * r + 512 * hh:1024 * r + 512 * hh + 512], src, "d%d" % r, off_mask)
+
+    if core == relay.get(li):
+        wait("p", ("lst", bits(off_mask)))
+        send([fl["S"]], T.lsf[:], T.lst[:], "lsf", off_mask)
+        for n in range(8):
+            way, t, hh = halves[n]
+            if way == "x":
+                k = spot("x", n)
+                forward(T.rly[:, 512 * k:512 * k + 512], li, t, hh, "rx%d" % k, off_mask)
+        wait("p", ("ls", cnt["ls"]))
+        return
+
     V, S = g.vector, g.scalar
 
     def ts(out, in0, s1, s2, o0, o1=None):
@@ -179,58 +234,61 @@ def rank_program(g, core, T, topo):
     if is_rank:
         for k in range(8):
             tok_idx = dma("s" if k % 2 == 0 else "a", "dix", T.lst[16 * k:16 * k + 16, :], T.idx[:])
-        tok_map = [dma("s", "dm%d" % h, piece(h), T.mp[:, hw * h:hw * h + hw]) for h in range(NP)]
+        tok_mi = [dma("s", "dm%d" % h, T.mi[:, pw * h:pw * h + pw], T.mp[:, hw * h:hw * h + hw]) for h in range(NP)]
 
     k_pcol = op("p", [], lambda: g.iota(T.pi[:, 2:3], [[0, 1]], 0, 1))
     k_it2 = op("p", [], lambda: g.iota(T.pi[:, 3:5], [[128, 2]], 0, 0))
     k_it16 = op("p", [], lambda: g.iota(T.it16[:], [[1, 16]], 0, 0, allow_small_or_imprecise_dtypes=True))
-    k_z = op("v", [], lambda: V.memset(T.win[:, Z:Z + 4], 0))
+    k_z = op("v", [], lambda: V.memset(T.win[:, Z:Z + 4], 0.0))
     k_r = op("v", [], lambda: V.memset(T.rs16[:], 1.0))
-    if is_sorter or is_rank:
-        k_ones = op("v", [], lambda: V.memset(T.ones[:], 1.0))
-    if is_sorter:
-        k_neg = op("v", [], lambda: V.memset(T.neg[:], -1.0))
-        k_q = op("v", [], lambda: V.memset(T.rs32[:], 1.0))
+    k_ones = op("v", [], lambda: V.memset(T.ones[:], 1.0))
+    k_neg = op("v", [], lambda: V.memset(T.neg[:], -1.0))
+    k_q = op("v", [], lambda: V.memset(T.rs32[:], 1.0))
+    k_onef = op("v", [], lambda: V.memset(T.onef[:], 1.0))
+    k_ls = op("v", [], lambda: V.memset(T.LS[:], 0.0))
     k_a = op("v", [k_pcol], lambda: ts(T.pi[:, 0:1], T.pi[:, 2:3], 15, None, A.bitwise_and))
     k_b = op("v", [k_pcol], lambda: ts(T.pi[:, 1:2], T.pi[:, 2:3], 4, None, A.logical_shift_right))
     k_pf = op("v", [k_a, k_b], lambda: V.tensor_copy(T.pf[:, 0:2], T.pi[:, 0:2]))
     k_rs16 = op("v", [k_r], lambda: V.memset(T.rs16[:, 0::16], 0.0))
-    if is_sorter:
-        k_rs32 = op("v", [k_q], lambda: V.memset(T.rs32[:, 0::32], 0.0))
+    k_rs32 = op("v", [k_q], lambda: V.memset(T.rs32[:, 0::32], 0.0))
     k_colf = op("v", [k_pf], lambda: ts(T.pf[:, 2:3], T.pf[:, 0:1], 8.0, T.pf[:, 1:2], A.mult, A.add))
     k_gkey = op("v", [k_pf], lambda: ts(T.pf[:, 3:4], T.pf[:, 1:2], float(gi << 19), None, A.add))
     k_s = op("v", [k_pf, k_it16], lambda: ts(T.smat[:], T.it16[:], T.pf[:, 0:1], None, A.is_equal))
     k_offe = op("v", [k_colf, k_it2], lambda: ts(T.offe[:], T.pi[:, 3:5], T.pf[:, 2:3], None, A.add))
 
     if is_rank:
+        tok_map = [op("v", [tok_mi[h]], lambda: V.tensor_copy(piece(h), T.mi[:, pw * h:pw * h + pw])) for h in range(NP)]
         wait("p", tok_idx)
         if is_sorter:
             send([fl["S"]], T.lsf[:], T.lst[:], "lsf", off_mask)
-        send([me["Q"]], T.lst[:], T.lst[:], "lst", on_mask)
+            send([me["Q"]], T.lst[:], T.lst[:], "lst", on_mask)
+        else:
+            send([relay[li]], T.lst[:], T.lst[:], "lst", off_mask)
         for h in range(NP):
             wait("p", tok_map[h])
             send([me["Q"]], piece(h), piece(h), "m%d%d" % (li, h), on_mask, "ms")
         part = T.win[:, 2048 * li:2048 * li + 2048]
         send([lanes[(li + k) % nl]["R"] for k in range(1, nl)], part, part, "m%d0" % li, on_mask, "ms")
     else:
-        if is_sorter:
-            wait("p", ("lst", bits(on_mask)))
-            send([fl["S"]], T.lsf[:], T.lst[:], "lsf", off_mask)
         for h in range(NP):
             wait("p", ("m%d%d" % (li, h), bits(on_mask)))
             send([lanes[(li + k) % nl]["Q"] for k in range(1, nl)], piece(h), piece(h), "m%d%d" % (li, h), on_mask)
     if is_rank:
         wait("s", ("ms", cnt["ms"]))
-        tok_tab = dma("s", "dtab", T.tw[:], T.tab[:])
+        dma("s", "dtab", T.tw[:, 0:HT], T.tab[:, 0:HT])
 
-    if is_sorter or is_rank:
+    k_ith = op("p", [], lambda: g.iota(T.ith[:, 0:64], [[1, 64]], 1 + 16 * half_r[0], 0,
+                                       allow_small_or_imprecise_dtypes=True))
+    k_itl = op("p", [], lambda: g.iota(T.ith[:, 64:128], [[1, 64]], 0, 0, allow_small_or_imprecise_dtypes=True))
+    k_base = op("p", [], lambda: g.iota(T.base[0:1, :], [[1024, nl], [0, 32]], 64 + 1024 * half_r[0], 0,
+                                        allow_small_or_imprecise_dtypes=True))
+    k_tri = op("p", [k_neg], lambda: g.affine_select(T.tri[:], T.neg[:], [[-1, 128]], A.is_ge, 0.0, 0, 1))
+    if is_rank:
+        k_repf = op("p", [k_onef], lambda: g.affine_select(T.repf[:], T.onef[:], [[0, 8], [-1, 16]], A.is_equal, 0.0,
+                                                           -16 * li, 1))
+    if is_sorter:
         k_rep = op("p", [k_ones], lambda: g.affine_select(T.rep[:], T.ones[:], [[-16, 8], [0, 8], [-1, 16]], A.is_equal,
                                                           0.0, 0, 1))
-    if is_sorter:
-        k_it = op("p", [], lambda: g.iota(T.it128[:], [[1, 128]], 0, 0, allow_small_or_imprecise_dtypes=True))
-        k_base = op("p", [], lambda: g.iota(T.base[0:1, :], [[1024, 8], [0, 32]], 0, 0,
-                                            allow_small_or_imprecise_dtypes=True))
-        k_tri = op("p", [k_neg], lambda: g.affine_select(T.tri[:], T.neg[:], [[-1, 128]], A.is_ge, 0.0, 0, 1))
 
     ls = T.lsf if is_sorter else T.lst
     if is_sorter:
@@ -251,25 +309,29 @@ def rank_program(g, core, T, topo):
     k_off1 = op("v", [d], lambda: ts(T.off1[:], T.tf[:, 768:1024], float(Z), None, A.min))
     for t in range(16):
         k_oh = op("v", [e], lambda: ts(T.oh[:, t::16], T.em[:], float((t >> 3) + ((t & 7) << (4 + CB))), None, A.is_equal))
-    if is_sorter or is_rank:
+    if is_sorter:
         k_rep7 = op("v", [k_rep], lambda: ts(T.rep7[:], T.rep[:], 128.0, None, A.mult))
 
+    maps = []
     for i in range(nl):
         for h in range(NP):
             if is_rank and i == li:
-                wait("v", tok_map[h])
+                maps.append(tok_map[h])
             elif not is_rank or h == 0:
-                wait("v", ("m%d%d" % (i, h), bits(on_mask)))
+                maps.append(("m%d%d" % (i, h), bits(on_mask)))
     n0 = 0
     pv = [T.pv0, T.pv1]
     half = [None, None]
-    for n in (256, 768, 1024, 1024, 1024):
-        tg = op("v", [k_off1, k_z], lambda: V.tensor_copy(
-            T.gat[:, n0:n0 + n], T.win[:, 0:Z + 4].indirect(T.off1[:, n0 // 16:(n0 + n) // 16])))
+    for q, n in (("v", 256), ("a", 512), ("v", 768), ("a", 768), ("v", 768), ("a", 512), ("v", 512)):
+        out, win, off = T.og[:, n0:n0 + n], T.win[:, 0:Z + 4], T.off1[:, n0 // 16:(n0 + n) // 16]
+        if q == "v":
+            tg = op("v", [k_off1, k_z] + maps, lambda: V.tensor_copy(out, win.indirect(off)))
+        else:
+            tg = op("a", [k_off1, k_z] + maps, lambda: S.activation(out, win.indirect(off), AF.Copy))
         for k in range(n0 // 128, (n0 + n) // 128):
             c0 = 16 * (k % SEL)
             half[k // SEL] = op("t", [tg, k_s], lambda: g.tensor.matmul(
-                pv[k // SEL][:, c0:c0 + 16], T.gat[:, 128 * k:128 * k + 128], T.smat[:], True, True))
+                pv[k // SEL][:, c0:c0 + 16], T.og[:, 128 * k:128 * k + 128], T.smat[:], True, True))
         n0 += n
     for h in range(2):
         w0, w1 = (0, 16 * SEL) if h == 0 else (16 * SEL, 512)
@@ -280,71 +342,77 @@ def rank_program(g, core, T, topo):
         k_res = op("v", [x], lambda: V.tensor_copy(T.res[:, w0 // 16:w1 // 16], T.xs[:, w0 + 15:w1:16]))
     wait("p", k_res)
     if is_sorter:
-        send([fl["S"]], T.rb[:], T.res[:], "rf", off_mask)
+        send([fl["S"], fl["H"]], T.rb[:], T.res[:], "rf", off_mask, "as")
     else:
-        send([me["S"]], T.ra[:], T.res[:], "rh", on_mask)
+        send([me["S"]], T.ra[:], T.res[:], "rh", on_mask, "as")
+    if is_rank:
+        wait("s", ("as", cnt["as"]))
+        tok_tab = dma("s", "dtab", T.tw[:, HT:8192], T.tab[:, HT:8192])
 
     if is_sorter:
         k_v = op("v", [("rh", bits(on_mask)), ("rf", bits(off_mask))],
                  lambda: V.tensor_tensor(T.vi[:], T.ra[:], T.rb[:], A.add))
-        k_o = op("v", [k_v], lambda: ts(T.o2[:], T.vi[:], 13, None, A.logical_shift_right))
-        for o in range(8):
-            k_m = op("v", [k_o], lambda: ts(T.msk[:, 32 * o:32 * o + 32], T.o2[:], float(o), None, A.is_equal))
-        k_sc = op("v", [k_m, k_rs32], lambda: V.tensor_tensor_scan(T.scn[:], T.rs32[:], T.msk[:], 0.0, A.mult, A.add))
-        x0 = op("v", [], lambda: ts(T.ib[:, 0:32], T.vi[:], 7, 63, A.logical_shift_right, A.bitwise_and))
-        x1 = op("v", [], lambda: ts(T.ib[:, 32:64], T.vi[:], 127, None, A.bitwise_and))
-        k_f0 = op("v", [x0, x1], lambda: V.tensor_copy(T.fb[:, 0:64], T.ib[:, 0:64]))
-        op("t", [k_base, k_ones], lambda: g.tensor.matmul(T.prk[:, 0:256], T.ones[0:1, 0:128], T.base[0:1, :], True, False))
-        op("t", [k_m, k_tri], lambda: g.tensor.matmul(T.prk[:, 0:256], T.tri[:], T.msk[:], False, False))
-        k_rk = op("t", [k_sc], lambda: g.tensor.matmul(T.prk[:, 0:256], T.ones[:, 0:128], T.scn[:], False, True))
-        x = op("v", [k_rk], lambda: V.tensor_tensor(T.pm[:], T.prk[:, 0:256], T.msk[:], A.mult))
-        x = op("v", [x], lambda: V.tensor_tensor(T.ss[:, 0:128], T.pm[:, 0:128], T.pm[:, 128:256], A.add))
-        k_n0 = op("v", [k_f0], lambda: ts(T.nb[:, 0:64], T.fb[:, 0:64], -1.0, None, A.mult))
-        x = op("v", [x], lambda: V.tensor_tensor(T.ss[:, 128:192], T.ss[:, 0:64], T.ss[:, 64:128], A.add))
-        k_pos = op("v", [x], lambda: V.tensor_tensor(T.pos[:], T.ss[:, 128:160], T.ss[:, 160:192], A.add))
-        op("v", [k_pos], lambda: ts(T.ib[:, 64:96], T.pos[:], 6, None, A.logical_shift_right))
-        x = op("v", [], lambda: ts(T.ib[:, 96:128], T.pos[:], 63, None, A.bitwise_and))
-        k_f1 = op("v", [x], lambda: V.tensor_copy(T.fb[:, 64:128], T.ib[:, 64:128]))
-        k_n1 = op("v", [k_f1], lambda: ts(T.nb[:, 64:128], T.fb[:, 64:128], -1.0, None, A.mult))
-        for k in range(SPLIT, 32):
-            w = 192 * (k - SPLIT)
-            op("a", [k_n1, k_n0, k_it], lambda: S.activation(T.ab[:, w:w + 128], T.it128[:], AF.Abs,
-                                                             bias=T.nb[:, 64 + k:65 + k]))
-            k_ab = op("a", [], lambda: S.activation(T.ab[:, w + 128:w + 192], T.it128[:, 0:64], AF.Abs,
-                                                    bias=T.nb[:, 96 + k:97 + k]))
-        done = []
-        for k in range(SPLIT, 32):
-            w, lo = 192 * (k - SPLIT), 128 * k
-            op("a", [k_ab], lambda: S.activation(T.lhs[:, lo:lo + 128], T.ab[:, w:w + 128], AF.Relu, bias=1.0, scale=-1.0))
-            op("a", [], lambda: S.activation(T.rhs[:, lo:lo + 64], T.ab[:, w + 128:w + 192], AF.Relu,
-                                             bias=T.fb[:, k:k + 1], scale=T.nb[:, k:k + 1]))
-            done.append(op("a", [], lambda: S.activation(T.rhs[:, lo + 64:lo + 128], T.ab[:, w + 128:w + 192], AF.Relu,
-                                                         bias=T.fb[:, 32 + k:33 + k], scale=T.nb[:, 32 + k:33 + k])))
-        for k in range(32):
-            lo = 128 * k
-            if k < SPLIT:
-                op("v", [k_f1, k_f0, k_it], lambda: ts(T.lhs[:, lo:lo + 128], T.it128[:], T.fb[:, 64 + k:65 + k], None,
-                                                       A.is_equal))
-                op("v", [], lambda: ts(T.rhs[:, lo:lo + 64], T.it128[:, 0:64], T.fb[:, 96 + k:97 + k], T.fb[:, k:k + 1],
+    else:
+        k_v = op("v", [k_res, ("rf", bits(off_mask))], lambda: V.tensor_tensor(T.vi[:], T.res[:], T.rb[:], A.add))
+    k_o = op("v", [k_v], lambda: ts(T.o2[:], T.vi[:], 13, None, A.logical_shift_right))
+    x0 = op("v", [], lambda: ts(T.ib[:, 0:32], T.vi[:], 8191, None, A.bitwise_and))
+    wait("v", k_o)
+    for o in range(nl):
+        k_m = op("v", [], lambda: ts(T.msk[:, 32 * o:32 * o + 32], T.o2[:], float(half_r[o]), None, A.is_equal))
+    k_sc = op("v", [k_m, k_rs32], lambda: V.tensor_tensor_scan(T.scn[:], T.rs32[:], T.msk[:], 0.0, A.mult, A.add))
+    k_f0 = op("v", [x0], lambda: V.tensor_copy(T.fb[:, 0:32], T.ib[:, 0:32]))
+    op("t", [k_base, k_ones], lambda: g.tensor.matmul(T.prk[:, 0:128], T.ones[0:1, 0:128], T.base[0:1, :], True, False))
+    op("t", [k_m, k_tri], lambda: g.tensor.matmul(T.prk[:, 0:128], T.tri[:], T.msk[:], False, False))
+    k_rk = op("t", [k_sc], lambda: g.tensor.matmul(T.prk[:, 0:128], T.ones[:, 0:128], T.scn[:], False, True))
+    k_n0 = op("v", [k_f0], lambda: ts(T.nb[:, 0:32], T.fb[:, 0:32], -1.0, None, A.mult))
+    x = op("v", [k_rk], lambda: V.tensor_tensor(T.pm[:, 0:128], T.prk[:, 0:128], T.msk[:], A.mult))
+    x = op("v", [x], lambda: V.tensor_tensor(T.pm[:, 128:192], T.pm[:, 0:64], T.pm[:, 64:128], A.add))
+    k_pos = op("v", [x], lambda: V.tensor_tensor(T.pos[:], T.pm[:, 128:160], T.pm[:, 160:192], A.add))
+    op("v", [k_pos], lambda: ts(T.ib[:, 32:64], T.pos[:], 6, None, A.logical_shift_right))
+    x = op("v", [], lambda: ts(T.ib[:, 64:96], T.pos[:], 63, None, A.bitwise_and))
+    k_f1 = op("v", [x], lambda: V.tensor_copy(T.fb[:, 32:96], T.ib[:, 32:96]))
+    k_n1 = op("v", [k_f1], lambda: ts(T.nb[:, 32:96], T.fb[:, 32:96], -1.0, None, A.mult))
+    for k in range(SPLIT, 32):
+        w = 128 * (k - SPLIT)
+        op("a", [k_n1, k_n0, k_ith, k_itl], lambda: S.activation(T.ab[:, w:w + 64], T.ith[:, 0:64], AF.Abs,
+                                                                 bias=T.nb[:, 32 + k:33 + k]))
+        k_ab = op("a", [], lambda: S.activation(T.ab[:, w + 64:w + 128], T.ith[:, 64:128], AF.Abs,
+                                                bias=T.nb[:, 64 + k:65 + k]))
+    done = []
+    for k in range(SPLIT, 32):
+        w, lo = 128 * (k - SPLIT), 64 * k
+        op("a", [k_ab], lambda: S.activation(T.lhs[:, lo:lo + 64], T.ab[:, w:w + 64], AF.Relu, bias=1.0, scale=-1.0))
+        done.append(op("a", [], lambda: S.activation(T.rhs[:, lo:lo + 64], T.ab[:, w + 64:w + 128], AF.Relu,
+                                                     bias=T.fb[:, k:k + 1], scale=T.nb[:, k:k + 1])))
+    for k in range(32):
+        lo = 64 * k
+        if k < SPLIT:
+            op("v", [k_f1, k_f0, k_ith, k_itl], lambda: ts(T.lhs[:, lo:lo + 64], T.ith[:, 0:64], T.fb[:, 32 + k:33 + k],
+                                                           None, A.is_equal))
+            x = op("v", [], lambda: ts(T.rhs[:, lo:lo + 64], T.ith[:, 64:128], T.fb[:, 64 + k:65 + k], T.fb[:, k:k + 1],
                                        A.is_equal, A.mult))
-                x = op("v", [], lambda: ts(T.rhs[:, lo + 64:lo + 128], T.it128[:, 0:64], T.fb[:, 96 + k:97 + k],
-                                           T.fb[:, 32 + k:33 + k], A.is_equal, A.mult))
-            else:
-                x = done[k - SPLIT]
-            k_l = op("t", [x], lambda: g.tensor.matmul(T.pl[:, 0:128], T.lhs[:, lo:lo + 128], T.rhs[:, lo:lo + 128],
-                                                       k == 0, k == 31))
-        slot = T.LL[:, 128 * myr:128 * myr + 128]
-        k_ll = op("v", [k_l], lambda: V.tensor_copy(slot, T.pl[:, 0:128]))
-        wait("p", k_ll)
-        send([flanes[(li - k) % nl]["R"] for k in range(nl)], slot, slot, "L%d" % myr, off_mask)
+        else:
+            x = done[k - SPLIT]
+        k_l = op("t", [x], lambda: g.tensor.matmul(T.pl[0:64, 0:64], T.lhs[:, lo:lo + 64], T.rhs[:, lo:lo + 64],
+                                                   k == 0, k == 31))
+    k_ll = op("v", [k_l, k_ls], lambda: V.tensor_copy(T.LS[0:64, :], T.pl[0:64, 0:64]))
+    slot = T.LL[:, 64 * myr:64 * myr + 64]
+    wait("p", k_ll)
+    if is_sorter:
+        send([flanes[(li - k) % nl]["R"] for k in range(nl)], slot, T.LS[:], "L%d" % myr, off_mask)
+    else:
         near = [lanes[(li - 1 - k) % nl]["R"] for k in range(nl)]
-        send([d for d in near if d != core], slot, slot, "L%d" % myr, side_mask)
+        send([d for d in near if d != core], slot, T.LS[:], "L%d" % myr, side_mask)
+        send([me["S"]], T.pz[:, 0:32], T.pos[:], "ph", side_mask)
 
     def order_offsets():
-        x0 = op("v", [k_pos], lambda: ts(T.qi[:, 0:32], T.pos[:], 10, None, A.logical_shift_right))
-        x1 = op("v", [], lambda: ts(T.qi[:, 32:64], T.pos[:], 7, None, A.bitwise_and))
-        x2 = op("v", [], lambda: ts(T.qi[:, 64:96], T.pos[:], 3, 7, A.logical_shift_right, A.bitwise_and))
-        x3 = op("v", [], lambda: ts(T.qi[:, 96:128], T.pos[:], 6, 15, A.logical_shift_right, A.bitwise_and))
+        x = op("v", [k_pos, ("ph", bits(side_mask))], lambda: V.tensor_tensor(T.pz[:, 32:64], T.pos[:], T.pz[:, 0:32], A.add))
+        x = op("v", [x], lambda: ts(T.pz[:, 64:96], T.pz[:, 32:64], 64.0, None, A.subtract))
+        at = T.pz[:, 64:96]
+        x0 = op("v", [x], lambda: ts(T.qi[:, 0:32], at, 10, None, A.logical_shift_right))
+        x1 = op("v", [], lambda: ts(T.qi[:, 32:64], at, 7, None, A.bitwise_and))
+        x2 = op("v", [], lambda: ts(T.qi[:, 64:96], at, 3, 7, A.logical_shift_right, A.bitwise_and))
+        x3 = op("v", [], lambda: ts(T.qi[:, 96:128], at, 6, 15, A.logical_shift_right, A.bitwise_and))
         op("v", [x0], lambda: ts(T.qf[:, 0:32], T.qi[:, 0:32], 8.0, None, A.mult))
         x = op("v", [x1], lambda: ts(T.qf[:, 32:64], T.qi[:, 32:64], 16.0, None, A.mult))
         k_qb = op("v", [x, x2, x3], lambda: V.tensor_tensor(T.qb[:], T.qf[:], T.qi[:, 64:128], A.add))
@@ -357,35 +425,32 @@ def rank_program(g, core, T, topo):
             y = op("v", [x], lambda: V.tensor_copy(T.off2[:, q::8], T.pv0[:, 32 * q:32 * q + 32]))
         return y
 
-    def pieces(t):
-        return [(0, 512), (512, 1024)] if t == 0 else [(0, 1024)]
-
     if is_sorter and not is_rank:
         k_off2 = order_offsets()
         wait("p", k_off2)
         send([me["R"]], T.off2[:], T.off2[:], "off2", side_mask)
-        n = 0
-        for t in range(nl):
-            for lo, hi in pieces(t):
-                wait("p", ("rl%d" % n, bits(on_mask)))
-                send([flanes[(li + t) % nl]["R"]], T.land[:, 1024 * myr + lo:1024 * myr + hi],
-                     T.rly[:, 1024 * t + lo:1024 * t + hi], "d%d" % myr, off_mask)
-                n += 1
+        own = [n for n in range(8) if halves[n][0] == "q"]
+        helped = ported[portless.index(li)]
+        more = [n for n in range(8) if PORT[n] == "k"]
+        todo = [(n, "rl", k, li) for k, n in enumerate(own)] + [(n, "rk", k, helped) for k, n in enumerate(more)]
+        for n, sem, k, lane in sorted(todo):
+            c = k if sem == "rl" else len(own) + k
+            forward(T.rly[:, 512 * c:512 * c + 512], lane, n // 2, n % 2, "%s%d" % (sem, k), side_mask)
 
     if is_rank:
         items = [("f", t, far_r[(li + t) % nl]) for t in range(nl)]
         items += [("n", t, near_r[(li + 1 + t) % nl]) for t in range(nl)]
         pr = [T.pr0, T.pr1, T.pr2, T.pr3]
-        w = slice(128 * myr, 128 * myr + 128)
         back, tok = {}, {}
 
         def spread(j):
             kind, t, r = items[j]
-            dep = k_ll if (r == myr and is_sorter) else ("L%d" % r, bits(off_mask if kind == "f" else side_mask))
-            op("t", [dep, back.get(j - 4), k_rep7], lambda: g.tensor.matmul(
-                pr[j % 4][:, 0:64], T.rep7[:, w], T.LL[:, 128 * r:128 * r + 64], True, False))
-            x = op("t", [], lambda: g.tensor.matmul(pr[j % 4][:, 0:64], T.rep[:, w],
-                                                    T.LL[:, 128 * r + 64:128 * r + 128], False, True))
+            own = r == myr and not is_sorter
+            dep = k_ll if own else ("L%d" % r, bits(off_mask if kind == "f" else side_mask))
+            part = T.LS if own else T.LL
+            c0 = 0 if own else 64 * r
+            x = op("t", [dep, back.get(j - 4), k_repf], lambda: g.tensor.matmul(
+                pr[j % 4][:, 0:64], T.repf[0:64, :], part[0:64, c0:c0 + 64], True, True))
             back[j] = op("v", [x], lambda: V.tensor_copy(T.offr[:, 64 * r:64 * r + 64], pr[j % 4][:, 0:64]))
 
         def gather(q, j, lo=0, hi=1024):
@@ -397,34 +462,42 @@ def rank_program(g, core, T, topo):
             else:
                 tok[(j, lo)] = op("a", [back[j], tok_tab], lambda: S.activation(out, T.tw[:, 0:8192].indirect(off), AF.Copy))
 
-        npc = [0]
-
-        def ship(j, lo=0, hi=1024):
+        def ship_near(j):
             kind, t, r = items[j]
-            wait("p", tok[(j, lo)])
-            src, dst = T.og[:, 1024 * j + lo:1024 * j + hi], T.land[:, 1024 * myr + lo:1024 * myr + hi]
-            if kind == "n":
-                send([cores[r]], dst, src, "d%d" % myr, side_mask if is_sorter else on_mask)
-            elif is_sorter:
-                send([cores[r]], dst, src, "d%d" % myr, off_mask)
+            wait("p", tok[(j, 0)])
+            way = (NEAR_PORT if is_sorter else NEAR_PORTLESS)[t]
+            send([cores[r]], T.land[:, 1024 * myr:1024 * myr + 1024], T.og[:, 1024 * j:1024 * j + 1024], "d%d" % myr,
+                 off_mask if way == "o" else side_mask)
+
+        def ship_far(n):
+            way, t, hh = halves[n]
+            kind, t, r = items[t]
+            wait("p", tok.get((t, 512 * hh), tok[(t, 0)]))
+            src = T.og[:, 1024 * t + 512 * hh:1024 * t + 512 * hh + 512]
+            if way == "d":
+                send([cores[r]], T.land[:, 1024 * myr + 512 * hh:1024 * myr + 512 * hh + 512], src, "d%d" % myr, off_mask)
+                return
+            k = spot(way, n)
+            if way == "x":
+                send([relay[li]], T.rly[:, 512 * k:512 * k + 512], src, "rx%d" % k, off_mask)
+            elif way == "q":
+                send([me["Q"]], T.rly[:, 512 * k:512 * k + 512], src, "rl%d" % k, side_mask)
             else:
-                send([me["Q"]], T.rly[:, 1024 * t + lo:1024 * t + hi], src, "rl%d" % npc[0], on_mask)
-                npc[0] += 1
+                c = PORTLESS.count("q") + k
+                send([lanes[portless[ported.index(li)]]["Q"]], T.rly[:, 512 * c:512 * c + 512], src, "rk%d" % k, side_mask)
 
         spread(0)
         gather("v", 0, 0, 512)
         spread(1)
         gather("v", 0, 512, 1024)
-        gather("a", 1)
+        gather("a", 1, 0, 512)
+        gather("a", 1, 512, 1024)
         spread(2)
         spread(3)
         gather("v", 2)
         gather("a", 3)
-        ship(0, 0, 512)
-        ship(0, 512, 1024)
-        ship(1)
-        ship(2)
-        ship(3)
+        for n in range(8):
+            ship_far(n)
         spread(4)
         spread(5)
         gather("v", 4)
@@ -434,7 +507,7 @@ def rank_program(g, core, T, topo):
         gather("v", 6)
         gather("a", 7)
         for j in range(4, 7):
-            ship(j)
+            ship_near(j)
         k_own = tok[(7, 0)]
 
     if is_rank:
@@ -442,10 +515,9 @@ def rank_program(g, core, T, topo):
         last = [k_off2, k_own]
         for i in range(nl):
             if i != li:
-                has_port = lanes[i]["R"] == lanes[i]["S"]
-                last.append(("d%d" % near_r[i], bits(side_mask) if has_port else bits(on_mask)))
-            last.append(("d%d" % far_r[i], bits(off_mask) * len(pieces((li - i) % nl))))
-        for lo, n in ((0, 512), (512, 512), (1024, 1024)):
+                last.append(("d%d" % near_r[i], bits(side_mask)))
+            last.append(("d%d" % far_r[i], 2 * bits(off_mask)))
+        for lo, n in ((0, 256), (256, 768), (1024, 1024)):
             hi = 2048 + lo
             x = op("v", last, lambda: V.tensor_copy(T.yb[:, lo:lo + n],
                                                     T.land[:, 0:8192].indirect(T.off2[:, lo // 16:(lo + n) // 16])))

from concourse.bass import DstId, RemoteDMATransfer
from concourse.mybir import AluOpType, ActivationFunctionType

SIM = 112
NP = 2
CB = 10
Z = 8192
SEL = 24
SPLIT = 20
HT = 4096
PORTLESS = "xqxqqxqx"
PORT = "dkdddddd"
NEAR_PORTLESS = "sos"
NEAR_PORT = "sss"

SCRATCH = {
    "lst": ("sbuf", [128, 256], "int32"),
    "lsf": ("sbuf", [128, 256], "int32"),
    "mi": ("sbuf", [128, 2048], "int32"),
    "win": ("sbuf", [128, 8196], "float32"),
    "pi": ("sbuf", [128, 5], "int32"),
    "pf": ("sbuf", [128, 4], "float32"),
    "offe": ("sbuf", [128, 2], "uint16"),
    "it16": ("sbuf", [128, 16], "float32"),
    "smat": ("sbuf", [128, 16], "float32"),
    "rs16": ("sbuf", [128, 512], "float32"),
    "ti": ("sbuf", [128, 768], "int32"),
    "tf": ("sbuf", [128, 1024], "float32"),
    "off1": ("sbuf", [128, 256], "uint16"),
    "ei": ("sbuf", [128, 32], "int32"),
    "em": ("sbuf", [128, 32], "int32"),
    "oh": ("sbuf", [128, 512], "float32"),
    "xm": ("sbuf", [128, 512], "float32"),
    "xs": ("sbuf", [128, 512], "float32"),
    "res": ("sbuf", [128, 32], "float32"),
    "ra": ("sbuf", [128, 32], "float32"),
    "rb": ("sbuf", [128, 32], "float32"),
    "ith": ("sbuf", [128, 128], "float32"),
    "onef": ("sbuf", [128, 128], "float32"),
    "ones": ("sbuf", [128, 1024], "bfloat16"),
    "neg": ("sbuf", [128, 128], "bfloat16"),
    "tri": ("sbuf", [128, 128], "bfloat16"),
    "base": ("sbuf", [1, 128], "bfloat16"),
    "rs32": ("sbuf", [128, 128], "bfloat16"),
    "rep": ("sbuf", [128, 1024], "bfloat16"),
    "rep7": ("sbuf", [128, 1024], "bfloat16"),
    "repf": ("sbuf", [128, 128], "float32"),
    "vi": ("sbuf", [128, 32], "int32"),
    "o2": ("sbuf", [128, 32], "int32"),
    "ib": ("sbuf", [128, 96], "int32"),
    "fb": ("sbuf", [128, 96], "float32"),
    "nb": ("sbuf", [128, 96], "float32"),
    "ab": ("sbuf", [128, 1536], "float32"),
    "msk": ("sbuf", [128, 128], "bfloat16"),
    "scn": ("sbuf", [128, 128], "bfloat16"),
    "pm": ("sbuf", [128, 192], "float32"),
    "pos": ("sbuf", [128, 32], "int32"),
    "pz": ("sbuf", [128, 96], "int32"),
    "lhs": ("sbuf", [128, 2048], "float32"),
    "rhs": ("sbuf", [128, 2048], "float32"),
    "LS": ("sbuf", [128, 64], "float32"),
    "LL": ("sbuf", [128, 512], "float32"),
    "qi": ("sbuf", [128, 128], "int32"),
    "qf": ("sbuf", [128, 64], "float32"),
    "qb": ("sbuf", [128, 64], "bfloat16"),
    "off2": ("sbuf", [128, 256], "uint16"),
    "tw": ("sbuf", [128, 8192], "float32"),
    "offr": ("sbuf", [128, 512], "uint16"),
    "og": ("sbuf", [128, 8192], "float32"),
    "land": ("sbuf", [128, 8192], "float32"),
    "rly": ("sbuf", [128, 4096], "float32"),
    "yb": ("sbuf", [128, 4096], "float32"),
    "pv0": ("psum", [128, 512], "float32"),
    "pv1": ("psum", [128, 512], "float32"),
    "prk": ("psum", [128, 512], "float32"),
    "pl": ("psum", [128, 512], "float32"),
    "pr0": ("psum", [128, 512], "float32"),
    "pr1": ("psum", [128, 512], "float32"),
    "pr2": ("psum", [128, 512], "float32"),
    "pr3": ("psum", [128, 512], "float32"),
}
SEMAPHORES = (["cv", "ct", "ca", "cp", "dix", "dy", "dtab", "lst", "lsf", "rh", "rf", "off2", "ph", "ls", "ms", "as"]
              + ["dm%d" % k for k in range(NP)]
              + ["m%d%d" % (i, h) for i in range(4) for h in range(NP)]
              + ["rl%d" % r for r in range(8)] + ["rk%d" % r for r in range(8)] + ["rx%d" % r for r in range(8)]
              + ["L%d" % r for r in range(8)] + ["d%d" % r for r in range(8)])


def _lanes(cores, chip, topo):
    far = [c for c in cores if topo.chip(c) != chip]
    idle = [c for c in range(SIM) if topo.chip(c) == chip and c not in cores]
    port = {c: all(topo.may_write(c, d) for d in far) for c in range(SIM) if topo.chip(c) == chip}
    with_port = [c for c in idle if port[c]]
    without = [c for c in idle if not port[c]]
    out = []
    for c in cores:
        if topo.chip(c) != chip:
            continue
        q = without.pop(0) if port[c] else with_port.pop(0)
        out.append({"R": c, "Q": q, "S": c if port[c] else q, "H": q if port[c] else c})
    return out


def _relays(cores, chips, gi, lanes, topo):
    out, used = {}, []
    far = [c for c in cores if topo.chip(c) == chips[1 - gi]]
    for li, l in enumerate(lanes):
        if l["R"] == l["S"]:
            continue
        best = None
        for x in range(SIM - 1, -1, -1):
            cx = topo.chip(x)
            if cx in chips or not topo.same_plane(cx, chips[gi]) or not all(topo.may_write(x, d) for d in far):
                continue
            key = ([topo.die(u) for u in used].count(topo.die(x)), [topo.chip(u) for u in used].count(cx))
            if best is None or key < best[0]:
                best = (key, x)
        out[li] = best[1]
        used.append(best[1])
    return out


def rank_program(g, core, T, topo):
    A = AluOpType
    AF = ActivationFunctionType
    cores = list(T.cores)
    chips = []
    for c in cores:
        if topo.chip(c) not in chips:
            chips.append(topo.chip(c))
    gi = li = None
    for k in range(2):
        ln = _lanes(cores, chips[k], topo)
        rx = _relays(cores, chips, k, ln, topo)
        for i in range(len(ln)):
            if core in (ln[i]["R"], ln[i]["Q"], rx.get(i)):
                gi, li = k, i
    if gi is None:
        return
    lanes = _lanes(cores, chips[gi], topo)
    flanes = _lanes(cores, chips[1 - gi], topo)
    relay = _relays(cores, chips, gi, lanes, topo)
    portless = [i for i in range(len(lanes)) if i in relay]
    ported = [i for i in range(len(lanes)) if i not in relay]
    me, fl = lanes[li], flanes[li]
    nl = len(lanes)
    is_rank = core == me["R"]
    is_sorter = core == me["S"]
    near_r = [cores.index(l["R"]) for l in lanes]
    far_r = [cores.index(l["R"]) for l in flanes]
    myr = cores.index(me["R"])
    half_r = far_r if is_sorter else near_r
    on_mask = topo.mask(me["R"], me["Q"])
    off_mask = topo.mask(me["S"], fl["S"])
    side_mask = on_mask & ~off_mask

    queues = {"v": g.vector, "t": g.tensor, "a": g.scalar, "p": g, "s": g.sync}
    cnt = {"cv": 0, "ct": 0, "ca": 0, "cp": 0, "ls": 0, "ms": 0, "as": 0}
    seen = {}

    def bits(m):
        return bin(m).count("1")

    def wait(q, *toks):
        for tok in toks:
            if tok is None:
                continue
            sem, val = tok
            if seen.get((q, sem), 0) < val:
                queues[q].wait_ge(T.sem[sem], val)
                seen[(q, sem)] = val

    def op(q, deps, f):
        wait(q, *deps)
        s = "c" + q
        f().then_inc(T.sem[s], 1)
        cnt[s] += 1
        return (s, cnt[s])

    def send(dsts, out, src, rsem, mask, lsem="ls"):
        if len(dsts) == 1:
            rid, pid, _ = topo.addr(dsts[0])
            g.remote_dma(out, src, T.sem[rsem], T.sem[lsem], pid, rid, mask)
        else:
            ids = []
            for d in dsts:
                rid, pid, _ = topo.addr(d)
                ids.append(DstId(rid=rid, pnc=pid))
            g.remote_dma_fused([RemoteDMATransfer(dst_ids=ids, dma_engine_mask=mask, remote_sem=T.sem[rsem],
                                                  srcs=[src], dsts=[out] * len(dsts))], local_sem=T.sem[lsem])
        cnt[lsem] += bits(mask)

    halves = [(way, n // 2, n % 2) for n, way in enumerate(PORT if li in ported else PORTLESS)]

    def spot(way, n):
        return [m for m in range(8) if halves[m][0] == way].index(n)

    def forward(src, lane, t, hh, sem, mask):
        r = cores.index(lanes[lane]["R"])
        wait("p", (sem, bits(mask)))
        send([flanes[(lane + t) % nl]["R"]], T.land[:, 1024 * r + 512 * hh:1024 * r + 512 * hh + 512], src, "d%d" % r, off_mask)

    if core == relay.get(li):
        wait("p", ("lst", bits(off_mask)))
        send([fl["S"]], T.lsf[:], T.lst[:], "lsf", off_mask)
        for n in range(8):
            way, t, hh = halves[n]
            if way == "x":
                k = spot("x", n)
                forward(T.rly[:, 512 * k:512 * k + 512], li, t, hh, "rx%d" % k, off_mask)
        wait("p", ("ls", cnt["ls"]))
        return

    V, S = g.vector, g.scalar

    def ts(out, in0, s1, s2, o0, o1=None):
        if o1 is None:
            return V.tensor_scalar(out, in0, s1, s2, o0)
        return V.tensor_scalar(out, in0, s1, s2, o0, o1)

    dma_tot = {}

    def dma(q, sem, out, in_):
        queues[q].dma_start(out, in_).then_inc(T.sem[sem], 16)
        dma_tot[sem] = dma_tot.get(sem, 0) + 16
        return (sem, dma_tot[sem])

    hw = 16384 // NP
    pw = 2048 // NP

    def piece(h):
        return T.win[:, 2048 * li + pw * h:2048 * li + pw * h + pw]

    if is_rank:
        for k in range(8):
            tok_idx = dma("s" if k % 2 == 0 else "a", "dix", T.lst[16 * k:16 * k + 16, :], T.idx[:])
        tok_mi = [dma("s", "dm%d" % h, T.mi[:, pw * h:pw * h + pw], T.mp[:, hw * h:hw * h + hw]) for h in range(NP)]

    k_pcol = op("p", [], lambda: g.iota(T.pi[:, 2:3], [[0, 1]], 0, 1))
    k_it2 = op("p", [], lambda: g.iota(T.pi[:, 3:5], [[128, 2]], 0, 0))
    k_it16 = op("p", [], lambda: g.iota(T.it16[:], [[1, 16]], 0, 0, allow_small_or_imprecise_dtypes=True))
    k_z = op("v", [], lambda: V.memset(T.win[:, Z:Z + 4], 0.0))
    k_r = op("v", [], lambda: V.memset(T.rs16[:], 1.0))
    k_ones = op("v", [], lambda: V.memset(T.ones[:], 1.0))
    k_neg = op("v", [], lambda: V.memset(T.neg[:], -1.0))
    k_q = op("v", [], lambda: V.memset(T.rs32[:], 1.0))
    k_onef = op("v", [], lambda: V.memset(T.onef[:], 1.0))
    k_ls = op("v", [], lambda: V.memset(T.LS[:], 0.0))
    k_a = op("v", [k_pcol], lambda: ts(T.pi[:, 0:1], T.pi[:, 2:3], 15, None, A.bitwise_and))
    k_b = op("v", [k_pcol], lambda: ts(T.pi[:, 1:2], T.pi[:, 2:3], 4, None, A.logical_shift_right))
    k_pf = op("v", [k_a, k_b], lambda: V.tensor_copy(T.pf[:, 0:2], T.pi[:, 0:2]))
    k_rs16 = op("v", [k_r], lambda: V.memset(T.rs16[:, 0::16], 0.0))
    k_rs32 = op("v", [k_q], lambda: V.memset(T.rs32[:, 0::32], 0.0))
    k_colf = op("v", [k_pf], lambda: ts(T.pf[:, 2:3], T.pf[:, 0:1], 8.0, T.pf[:, 1:2], A.mult, A.add))
    k_gkey = op("v", [k_pf], lambda: ts(T.pf[:, 3:4], T.pf[:, 1:2], float(gi << 19), None, A.add))
    k_s = op("v", [k_pf, k_it16], lambda: ts(T.smat[:], T.it16[:], T.pf[:, 0:1], None, A.is_equal))
    k_offe = op("v", [k_colf, k_it2], lambda: ts(T.offe[:], T.pi[:, 3:5], T.pf[:, 2:3], None, A.add))

    if is_rank:
        tok_map = [op("v", [tok_mi[h]], lambda: V.tensor_copy(piece(h), T.mi[:, pw * h:pw * h + pw])) for h in range(NP)]
        wait("p", tok_idx)
        if is_sorter:
            send([fl["S"]], T.lsf[:], T.lst[:], "lsf", off_mask)
            send([me["Q"]], T.lst[:], T.lst[:], "lst", on_mask)
        else:
            send([relay[li]], T.lst[:], T.lst[:], "lst", off_mask)
        for h in range(NP):
            wait("p", tok_map[h])
            send([me["Q"]], piece(h), piece(h), "m%d%d" % (li, h), on_mask, "ms")
        part = T.win[:, 2048 * li:2048 * li + 2048]
        send([lanes[(li + k) % nl]["R"] for k in range(1, nl)], part, part, "m%d0" % li, on_mask, "ms")
    else:
        for h in range(NP):
            wait("p", ("m%d%d" % (li, h), bits(on_mask)))
            send([lanes[(li + k) % nl]["Q"] for k in range(1, nl)], piece(h), piece(h), "m%d%d" % (li, h), on_mask)
    if is_rank:
        wait("s", ("ms", cnt["ms"]))
        dma("s", "dtab", T.tw[:, 0:HT], T.tab[:, 0:HT])

    k_ith = op("p", [], lambda: g.iota(T.ith[:, 0:64], [[1, 64]], 1 + 16 * half_r[0], 0,
                                       allow_small_or_imprecise_dtypes=True))
    k_itl = op("p", [], lambda: g.iota(T.ith[:, 64:128], [[1, 64]], 0, 0, allow_small_or_imprecise_dtypes=True))
    k_base = op("p", [], lambda: g.iota(T.base[0:1, :], [[1024, nl], [0, 32]], 64 + 1024 * half_r[0], 0,
                                        allow_small_or_imprecise_dtypes=True))
    k_tri = op("p", [k_neg], lambda: g.affine_select(T.tri[:], T.neg[:], [[-1, 128]], A.is_ge, 0.0, 0, 1))
    if is_rank:
        k_repf = op("p", [k_onef], lambda: g.affine_select(T.repf[:], T.onef[:], [[0, 8], [-1, 16]], A.is_equal, 0.0,
                                                           -16 * li, 1))
    if is_sorter:
        k_rep = op("p", [k_ones], lambda: g.affine_select(T.rep[:], T.ones[:], [[-16, 8], [0, 8], [-1, 16]], A.is_equal,
                                                          0.0, 0, 1))

    ls = T.lsf if is_sorter else T.lst
    if is_sorter:
        have = ("lsf", bits(off_mask))
    elif is_rank:
        have = tok_idx
    else:
        have = ("lst", bits(on_mask))
    a = op("v", [have], lambda: ts(T.ti[:, 0:256], ls[:], 1, 7 | (1 << 19), A.logical_shift_right, A.bitwise_and))
    b = op("v", [], lambda: ts(T.ti[:, 256:512], ls[:], 7 + CB, 4 * NP - 1, A.logical_shift_right, A.bitwise_and))
    c = op("v", [], lambda: ts(T.ti[:, 512:768], ls[:], 4, (1 << CB) - 1, A.logical_shift_right, A.bitwise_and))
    e = op("v", [k_offe], lambda: V.tensor_copy(T.ei[:], ls[:, 0:256].indirect(T.offe[:, 0:2])))
    a = op("v", [a, k_gkey], lambda: ts(T.tf[:, 0:256], T.ti[:, 0:256], T.pf[:, 3:4], 16384.0, A.not_equal, A.mult))
    b = op("v", [b], lambda: ts(T.tf[:, 256:512], T.ti[:, 256:512], float(1 << CB), None, A.mult))
    e = op("v", [e], lambda: ts(T.em[:], T.ei[:], 1 | (7 << (4 + CB)), None, A.bitwise_and))
    c = op("v", [a, c], lambda: V.tensor_tensor(T.tf[:, 512:768], T.tf[:, 0:256], T.ti[:, 512:768], A.add))
    d = op("v", [c, b], lambda: V.tensor_tensor(T.tf[:, 768:1024], T.tf[:, 512:768], T.tf[:, 256:512], A.add))
    k_off1 = op("v", [d], lambda: ts(T.off1[:], T.tf[:, 768:1024], float(Z), None, A.min))
    for t in range(16):
        k_oh = op("v", [e], lambda: ts(T.oh[:, t::16], T.em[:], float((t >> 3) + ((t & 7) << (4 + CB))), None, A.is_equal))
    if is_sorter:
        k_rep7 = op("v", [k_rep], lambda: ts(T.rep7[:], T.rep[:], 128.0, None, A.mult))

    maps = []
    for i in range(nl):
        for h in range(NP):
            if is_rank and i == li:
                maps.append(tok_map[h])
            elif not is_rank or h == 0:
                maps.append(("m%d%d" % (i, h), bits(on_mask)))
    n0 = 0
    pv = [T.pv0, T.pv1]
    half = [None, None]
    for q, n in (("v", 256), ("a", 512), ("v", 768), ("a", 768), ("v", 768), ("a", 512), ("v", 512)):
        out, win, off = T.og[:, n0:n0 + n], T.win[:, 0:Z + 4], T.off1[:, n0 // 16:(n0 + n) // 16]
        if q == "v":
            tg = op("v", [k_off1, k_z] + maps, lambda: V.tensor_copy(out, win.indirect(off)))
        else:
            tg = op("a", [k_off1, k_z] + maps, lambda: S.activation(out, win.indirect(off), AF.Copy))
        for k in range(n0 // 128, (n0 + n) // 128):
            c0 = 16 * (k % SEL)
            half[k // SEL] = op("t", [tg, k_s], lambda: g.tensor.matmul(
                pv[k // SEL][:, c0:c0 + 16], T.og[:, 128 * k:128 * k + 128], T.smat[:], True, True))
        n0 += n
    for h in range(2):
        w0, w1 = (0, 16 * SEL) if h == 0 else (16 * SEL, 512)
        n = w1 - w0
        x = op("v", [half[h], k_oh], lambda: V.tensor_tensor(T.xm[:, w0:w1], pv[h][:, 0:n], T.oh[:, w0:w1], A.mult))
        x = op("v", [x, k_rs16], lambda: V.tensor_tensor_scan(T.xs[:, w0:w1], T.rs16[:, 0:n], T.xm[:, w0:w1], 0.0, A.mult,
                                                              A.add))
        k_res = op("v", [x], lambda: V.tensor_copy(T.res[:, w0 // 16:w1 // 16], T.xs[:, w0 + 15:w1:16]))
    wait("p", k_res)
    if is_sorter:
        send([fl["S"], fl["H"]], T.rb[:], T.res[:], "rf", off_mask, "as")
    else:
        send([me["S"]], T.ra[:], T.res[:], "rh", on_mask, "as")
    if is_rank:
        wait("s", ("as", cnt["as"]))
        tok_tab = dma("s", "dtab", T.tw[:, HT:8192], T.tab[:, HT:8192])

    if is_sorter:
        k_v = op("v", [("rh", bits(on_mask)), ("rf", bits(off_mask))],
                 lambda: V.tensor_tensor(T.vi[:], T.ra[:], T.rb[:], A.add))
    else:
        k_v = op("v", [k_res, ("rf", bits(off_mask))], lambda: V.tensor_tensor(T.vi[:], T.res[:], T.rb[:], A.add))
    k_o = op("v", [k_v], lambda: ts(T.o2[:], T.vi[:], 13, None, A.logical_shift_right))
    x0 = op("v", [], lambda: ts(T.ib[:, 0:32], T.vi[:], 8191, None, A.bitwise_and))
    wait("v", k_o)
    for o in range(nl):
        k_m = op("v", [], lambda: ts(T.msk[:, 32 * o:32 * o + 32], T.o2[:], float(half_r[o]), None, A.is_equal))
    k_sc = op("v", [k_m, k_rs32], lambda: V.tensor_tensor_scan(T.scn[:], T.rs32[:], T.msk[:], 0.0, A.mult, A.add))
    k_f0 = op("v", [x0], lambda: V.tensor_copy(T.fb[:, 0:32], T.ib[:, 0:32]))
    op("t", [k_base, k_ones], lambda: g.tensor.matmul(T.prk[:, 0:128], T.ones[0:1, 0:128], T.base[0:1, :], True, False))
    op("t", [k_m, k_tri], lambda: g.tensor.matmul(T.prk[:, 0:128], T.tri[:], T.msk[:], False, False))
    k_rk = op("t", [k_sc], lambda: g.tensor.matmul(T.prk[:, 0:128], T.ones[:, 0:128], T.scn[:], False, True))
    k_n0 = op("v", [k_f0], lambda: ts(T.nb[:, 0:32], T.fb[:, 0:32], -1.0, None, A.mult))
    x = op("v", [k_rk], lambda: V.tensor_tensor(T.pm[:, 0:128], T.prk[:, 0:128], T.msk[:], A.mult))
    x = op("v", [x], lambda: V.tensor_tensor(T.pm[:, 128:192], T.pm[:, 0:64], T.pm[:, 64:128], A.add))
    k_pos = op("v", [x], lambda: V.tensor_tensor(T.pos[:], T.pm[:, 128:160], T.pm[:, 160:192], A.add))
    op("v", [k_pos], lambda: ts(T.ib[:, 32:64], T.pos[:], 6, None, A.logical_shift_right))
    x = op("v", [], lambda: ts(T.ib[:, 64:96], T.pos[:], 63, None, A.bitwise_and))
    k_f1 = op("v", [x], lambda: V.tensor_copy(T.fb[:, 32:96], T.ib[:, 32:96]))
    k_n1 = op("v", [k_f1], lambda: ts(T.nb[:, 32:96], T.fb[:, 32:96], -1.0, None, A.mult))
    for k in range(SPLIT, 32):
        w = 128 * (k - SPLIT)
        op("a", [k_n1, k_n0, k_ith, k_itl], lambda: S.activation(T.ab[:, w:w + 64], T.ith[:, 0:64], AF.Abs,
                                                                 bias=T.nb[:, 32 + k:33 + k]))
        k_ab = op("a", [], lambda: S.activation(T.ab[:, w + 64:w + 128], T.ith[:, 64:128], AF.Abs,
                                                bias=T.nb[:, 64 + k:65 + k]))
    done = []
    for k in range(SPLIT, 32):
        w, lo = 128 * (k - SPLIT), 64 * k
        op("a", [k_ab], lambda: S.activation(T.lhs[:, lo:lo + 64], T.ab[:, w:w + 64], AF.Relu, bias=1.0, scale=-1.0))
        done.append(op("a", [], lambda: S.activation(T.rhs[:, lo:lo + 64], T.ab[:, w + 64:w + 128], AF.Relu,
                                                     bias=T.fb[:, k:k + 1], scale=T.nb[:, k:k + 1])))
    for k in range(32):
        lo = 64 * k
        if k < SPLIT:
            op("v", [k_f1, k_f0, k_ith, k_itl], lambda: ts(T.lhs[:, lo:lo + 64], T.ith[:, 0:64], T.fb[:, 32 + k:33 + k],
                                                           None, A.is_equal))
            x = op("v", [], lambda: ts(T.rhs[:, lo:lo + 64], T.ith[:, 64:128], T.fb[:, 64 + k:65 + k], T.fb[:, k:k + 1],
                                       A.is_equal, A.mult))
        else:
            x = done[k - SPLIT]
        k_l = op("t", [x], lambda: g.tensor.matmul(T.pl[0:64, 0:64], T.lhs[:, lo:lo + 64], T.rhs[:, lo:lo + 64],
                                                   k == 0, k == 31))
    k_ll = op("v", [k_l, k_ls], lambda: V.tensor_copy(T.LS[0:64, :], T.pl[0:64, 0:64]))
    slot = T.LL[:, 64 * myr:64 * myr + 64]
    wait("p", k_ll)
    if is_sorter:
        send([flanes[(li - k) % nl]["R"] for k in range(nl)], slot, T.LS[:], "L%d" % myr, off_mask)
    else:
        near = [lanes[(li - 1 - k) % nl]["R"] for k in range(nl)]
        send([d for d in near if d != core], slot, T.LS[:], "L%d" % myr, side_mask)
        send([me["S"]], T.pz[:, 0:32], T.pos[:], "ph", side_mask)

    def order_offsets():
        x = op("v", [k_pos, ("ph", bits(side_mask))], lambda: V.tensor_tensor(T.pz[:, 32:64], T.pos[:], T.pz[:, 0:32], A.add))
        x = op("v", [x], lambda: ts(T.pz[:, 64:96], T.pz[:, 32:64], 64.0, None, A.subtract))
        at = T.pz[:, 64:96]
        x0 = op("v", [x], lambda: ts(T.qi[:, 0:32], at, 10, None, A.logical_shift_right))
        x1 = op("v", [], lambda: ts(T.qi[:, 32:64], at, 7, None, A.bitwise_and))
        x2 = op("v", [], lambda: ts(T.qi[:, 64:96], at, 3, 7, A.logical_shift_right, A.bitwise_and))
        x3 = op("v", [], lambda: ts(T.qi[:, 96:128], at, 6, 15, A.logical_shift_right, A.bitwise_and))
        op("v", [x0], lambda: ts(T.qf[:, 0:32], T.qi[:, 0:32], 8.0, None, A.mult))
        x = op("v", [x1], lambda: ts(T.qf[:, 32:64], T.qi[:, 32:64], 16.0, None, A.mult))
        k_qb = op("v", [x, x2, x3], lambda: V.tensor_tensor(T.qb[:], T.qf[:], T.qi[:, 64:128], A.add))
        for q in range(8):
            w = slice(128 * q, 128 * q + 128)
            op("t", [k_qb, k_rep7, k_res], lambda: g.tensor.matmul(T.pv0[:, 32 * q:32 * q + 32], T.rep7[:, w],
                                                                   T.qb[:, 0:32], True, False))
            x = op("t", [], lambda: g.tensor.matmul(T.pv0[:, 32 * q:32 * q + 32], T.rep[:, w], T.qb[:, 32:64], False, True))
        for q in range(8):
            y = op("v", [x], lambda: V.tensor_copy(T.off2[:, q::8], T.pv0[:, 32 * q:32 * q + 32]))
        return y

    if is_sorter and not is_rank:
        k_off2 = order_offsets()
        wait("p", k_off2)
        send([me["R"]], T.off2[:], T.off2[:], "off2", side_mask)
        own = [n for n in range(8) if halves[n][0] == "q"]
        helped = ported[portless.index(li)]
        more = [n for n in range(8) if PORT[n] == "k"]
        todo = [(n, "rl", k, li) for k, n in enumerate(own)] + [(n, "rk", k, helped) for k, n in enumerate(more)]
        for n, sem, k, lane in sorted(todo):
            c = k if sem == "rl" else len(own) + k
            forward(T.rly[:, 512 * c:512 * c + 512], lane, n // 2, n % 2, "%s%d" % (sem, k), side_mask)

    if is_rank:
        items = [("f", t, far_r[(li + t) % nl]) for t in range(nl)]
        items += [("n", t, near_r[(li + 1 + t) % nl]) for t in range(nl)]
        pr = [T.pr0, T.pr1, T.pr2, T.pr3]
        back, tok = {}, {}

        def spread(j):
            kind, t, r = items[j]
            own = r == myr and not is_sorter
            dep = k_ll if own else ("L%d" % r, bits(off_mask if kind == "f" else side_mask))
            part = T.LS if own else T.LL
            c0 = 0 if own else 64 * r
            x = op("t", [dep, back.get(j - 4), k_repf], lambda: g.tensor.matmul(
                pr[j % 4][:, 0:64], T.repf[0:64, :], part[0:64, c0:c0 + 64], True, True))
            back[j] = op("v", [x], lambda: V.tensor_copy(T.offr[:, 64 * r:64 * r + 64], pr[j % 4][:, 0:64]))

        def gather(q, j, lo=0, hi=1024):
            kind, t, r = items[j]
            out = T.land[:, 1024 * myr:1024 * myr + 1024] if r == myr else T.og[:, 1024 * j + lo:1024 * j + hi]
            off = T.offr[:, 64 * r + lo // 16:64 * r + hi // 16]
            if q == "v":
                tok[(j, lo)] = op("v", [back[j], tok_tab], lambda: V.tensor_copy(out, T.tw[:, 0:8192].indirect(off)))
            else:
                tok[(j, lo)] = op("a", [back[j], tok_tab], lambda: S.activation(out, T.tw[:, 0:8192].indirect(off), AF.Copy))

        def ship_near(j):
            kind, t, r = items[j]
            wait("p", tok[(j, 0)])
            way = (NEAR_PORT if is_sorter else NEAR_PORTLESS)[t]
            send([cores[r]], T.land[:, 1024 * myr:1024 * myr + 1024], T.og[:, 1024 * j:1024 * j + 1024], "d%d" % myr,
                 off_mask if way == "o" else side_mask)

        def ship_far(n):
            way, t, hh = halves[n]
            kind, t, r = items[t]
            wait("p", tok.get((t, 512 * hh), tok[(t, 0)]))
            src = T.og[:, 1024 * t + 512 * hh:1024 * t + 512 * hh + 512]
            if way == "d":
                send([cores[r]], T.land[:, 1024 * myr + 512 * hh:1024 * myr + 512 * hh + 512], src, "d%d" % myr, off_mask)
                return
            k = spot(way, n)
            if way == "x":
                send([relay[li]], T.rly[:, 512 * k:512 * k + 512], src, "rx%d" % k, off_mask)
            elif way == "q":
                send([me["Q"]], T.rly[:, 512 * k:512 * k + 512], src, "rl%d" % k, side_mask)
            else:
                c = PORTLESS.count("q") + k
                send([lanes[portless[ported.index(li)]]["Q"]], T.rly[:, 512 * c:512 * c + 512], src, "rk%d" % k, side_mask)

        spread(0)
        gather("v", 0, 0, 512)
        spread(1)
        gather("v", 0, 512, 1024)
        gather("a", 1, 0, 512)
        gather("a", 1, 512, 1024)
        spread(2)
        spread(3)
        gather("v", 2)
        gather("a", 3)
        for n in range(8):
            ship_far(n)
        spread(4)
        spread(5)
        gather("v", 4)
        gather("a", 5)
        spread(6)
        spread(7)
        gather("v", 6)
        gather("a", 7)
        for j in range(4, 7):
            ship_near(j)
        k_own = tok[(7, 0)]

    if is_rank:
        k_off2 = order_offsets() if is_sorter else ("off2", bits(side_mask))
        last = [k_off2, k_own]
        for i in range(nl):
            if i != li:
                last.append(("d%d" % near_r[i], bits(side_mask)))
            last.append(("d%d" % far_r[i], 2 * bits(off_mask)))
        for lo, n in ((0, 256), (256, 768), (1024, 1024)):
            hi = 2048 + lo
            x = op("v", last, lambda: V.tensor_copy(T.yb[:, lo:lo + n],
                                                    T.land[:, 0:8192].indirect(T.off2[:, lo // 16:(lo + n) // 16])))
            wait("s", x)
            dma("s", "dy", T.y[:, lo:lo + n], T.yb[:, lo:lo + n])
            x = op("a", last, lambda: S.activation(T.yb[:, hi:hi + n],
                                                   T.land[:, 0:8192].indirect(T.off2[:, hi // 16:(hi + n) // 16]), AF.Copy))
            wait("s", x)
            dma("s", "dy", T.y[:, hi:hi + n], T.yb[:, hi:hi + n])

    for s in sorted(cnt):
        if cnt[s]:
            wait("p", (s, cnt[s]))
    for s in sorted(dma_tot):
        wait("p", (s, dma_tot[s]))
